import numpy as np
import ml_dtypes


def mxq(x, axis, fmt="e4m3"):
    dtype, down = {"e4m3": (ml_dtypes.float8_e4m3fn, 7), "e5m2": (ml_dtypes.float8_e5m2, 14)}[fmt]
    v = np.moveaxis(np.asarray(x, np.float32).astype(ml_dtypes.bfloat16).astype(np.float64), axis, -1)
    blocks = v.reshape(v.shape[:-1] + (-1, 32))
    amax = np.abs(blocks).max(-1, keepdims=True)
    byte = np.maximum(np.where(amax > 0, np.frexp(amax)[1] - 1 + 127, 0) - down, 1)
    scale = np.exp2(byte - 127.0)
    codes = (blocks / scale).astype(np.float32).astype(dtype).astype(np.float64)
    return np.moveaxis((codes * scale).reshape(v.shape), -1, axis)


WIDE = False


def mx_kscale(k):
    if not WIDE:
        return np.ones(k)
    levels = np.array([10, -10, 5, -5, 0])
    if k % 512:
        return np.exp2(np.random.permutation(np.resize(levels, k // 32))).repeat(32)
    a = np.empty((k // 512, 16))
    for p in range(k // 512):
        a[p, :8] = np.random.permutation(np.resize(levels, 8))
        for g in range(8):
            far = levels[np.abs(levels - a[p, g]) >= 10]
            a[p, g + 8] = far[np.random.randint(len(far))]
    return np.exp2(a.ravel()).repeat(32)


def f64(x):
    return np.asarray(x).astype(np.float64)


def striped(idx):
    return np.tile(idx.reshape(-1, 16).T, (8, 1)).astype(np.uint16)


def unstriped(offs):
    return offs[:16].T.reshape(-1).astype(np.int64)


def pack_weight(w):
    k, n = w.shape
    w = f64(np.asarray(w, np.float32).astype(ml_dtypes.bfloat16)).reshape(k // 32, 32, n)
    amax = np.abs(w).max(1)
    byte = np.clip(np.where(amax > 0, np.frexp(amax)[1] - 1 + 127 - 7, 1), 1, 254)
    scaled = (w * np.exp2(127.0 - byte)[:, None, :]).reshape(k, n).astype(np.float32)
    words = np.ascontiguousarray(scaled.reshape(k // 512, 128, 4, n).transpose(0, 1, 3, 2)).astype(ml_dtypes.float8_e4m3fn).view(np.uint8)
    return words, np.ascontiguousarray(byte.astype(np.uint8).reshape(k // 512, 16, n))


def unpack_weight(words, scales):
    g, p, n, _ = words.shape
    vals = np.ascontiguousarray(words).view(ml_dtypes.float8_e4m3fn).astype(np.float64) * np.repeat(np.exp2(scales.astype(np.float64) - 127.0), 8, axis=1)[..., None]
    return vals.transpose(0, 1, 3, 2).reshape(g * 512, n)


def relu(v):
    return np.maximum(v, 0.0)


K, T, S, H, N, D = 512, 1024, 512, 512, 128, 2


def setup_inputs():
    n = np.random.standard_normal
    s = mx_kscale(K)[:, None]
    u = mx_kscale(H)
    packed_xT = pack_weight(n((K, T)) * s)
    return {
        "x_words": packed_xT[0],
        "x_scales": packed_xT[1],
        "w1": (n((K, H)) / np.sqrt(K) / s * u).astype(np.float32),
        "w2": (n((H, N)) / np.sqrt(H) / u[:, None]).astype(np.float32),
        "w3": (n((H, N)) / np.sqrt(H) / u[:, None]).astype(np.float32),
        "offs": striped(np.random.permutation(T)[:S]),
    }


def reference(x_words, x_scales, w1, w2, w3, offs):
    xq = unpack_weight(x_words, x_scales)[:, unstriped(offs)]
    h = relu(mxq(f64(w1), 0, "e4m3").T @ xq)
    y = mxq(f64(w2), 0, "e4m3").T @ mxq(h, 0, "e4m3")
    z = h.reshape(len(h), -1, D).max(axis=2)
    gg = mxq(f64(w3), 0, "e4m3").T @ mxq(z, 0, "e4m3")
    return y + np.repeat(gg, D, axis=1)

@@ -1,0 +1,156 @@
+from contextlib import ExitStack
+
+import concourse.mybir as mybir
+
+K, T, S, H, N = 512, 1024, 512, 512, 128
+FLOPS = 2 * K * H * S + 2 * H * N * S + 2 * H * N * (S // 2)
+
+F32 = mybir.dt.float32
+BF16 = mybir.dt.bfloat16
+I32 = mybir.dt.int32
+U32 = mybir.dt.uint32
+U16 = mybir.dt.uint16
+U8 = mybir.dt.uint8
+FP8X4 = mybir.dt.float8_e4m3fn_x4
+COPY = mybir.ActivationFunctionType.Copy
+RELU = mybir.ActivationFunctionType.Relu
+MAX = mybir.AluOpType.max
+
+P = 128
+CH = 128
+W1_SPLIT = 44
+
+
+def tile_picked_ypnseg_max_p_kernel(tc, x_words, x_scales, w1, w2, w3, offs, out):
+    nc = tc.nc
+    with ExitStack() as ctx:
+        sb = ctx.enter_context(tc.tile_pool(name="sb", bufs=1))
+        reuse = ctx.enter_context(tc.tile_pool(name="reuse", bufs=1))
+        ps = ctx.enter_context(tc.psum_pool(name="ps", bufs=1))
+
+        offsets = sb.tile([P, S // 16], U16, name="offsets")
+        xw = sb.tile([P, T], U32, name="xw", align_bytes=64)
+        xs = reuse.tile([P, T], U8, name="xs", align_bytes=64, offset=0)
+        w1_raw = [sb.tile([P, 4, H // 2], F32, name=f"w1_raw{h}", align_bytes=64) for h in range(2)]
+
+        w1_rows = w1.rearrange("(p j) c -> p j c", j=4)
+        nc.vector.memset(xs[:].bitcast(I32), 0)
+        nc.sync.dma_start(out=w1_raw[0][:], in_=w1_rows[:, :, 0 : H // 2])
+        nc.sync.dma_start(offsets[:], offs)
+        for q in range(4):
+            nc.scalar.dma_start(out=xs[32 * q : 32 * q + 4, :].bitcast(I32), in_=x_scales[0, 4 * q : 4 * q + 4, :].bitcast(I32))
+        nc.sync.dma_start(out=w1_raw[1][:], in_=w1_rows[:, :, H // 2 : H])
+        nc.sync.dma_start(out=xw[:].bitcast(I32), in_=x_words[0].rearrange("p n t -> p (n t)").bitcast(I32))
+
+        gs = sb.tile([P, S], U8, name="gs", align_bytes=64)
+        nc.vector.tensor_copy(gs[:], xs[:].indirect(offsets[:]))
+
+        w1_bf = [
+            sb.tile([P, 4, 64, 4], BF16, name="w1_bf0", align_bytes=64),
+            reuse.tile([P, 4, 64, 4], BF16, name="w1_bf1", align_bytes=64, offset=512),
+        ]
+        w1_q = sb.tile([P, H], U32, name="w1_q", align_bytes=64)
+        w1_s = reuse.tile([P, H], U8, name="w1_s", align_bytes=64, offset=0)
+
+        def w1_views(h, m0, m1):
+            dst = w1_bf[h][:].rearrange("p t m j -> p m t j")[:, m0:m1]
+            src = w1_raw[h][:].rearrange("p j (m t) -> p m t j", t=4)[:, m0:m1]
+            return dst, src
+
+        dst, src = w1_views(0, 0, 64)
+        nc.scalar.activation(dst, src, COPY)
+        w23_raw = sb.tile([P, 2, 4, N], F32, name="w1_raw0", align_bytes=64)
+        nc.sync.dma_start(out=w23_raw[:, 0], in_=w2.rearrange("(p j) c -> p j c", j=4))
+        nc.sync.dma_start(out=w23_raw[:, 1], in_=w3.rearrange("(p j) c -> p j c", j=4))
+        dst, src = w1_views(1, 0, W1_SPLIT)
+        nc.vector.tensor_copy(dst, src)
+        dst, src = w1_views(1, W1_SPLIT, 64)
+        nc.scalar.activation(dst, src, COPY)
+        for h in range(2):
+            for t in range(4):
+                cols = slice(128 * t + 64 * h, 128 * t + 64 * h + 64)
+                nc.vector.quantize_mx(
+                    out=w1_q[:, cols].bitcast(FP8X4), scales=w1_s[:, cols], in_=w1_bf[h][:, t].rearrange("p m j -> p (m j)")
+                )
+
+        gw = [sb.tile([P, CH], U32, name=f"gw{c}", align_bytes=64) for c in range(4)]
+        for c in range(4):
+            nc.vector.tensor_copy(gw[c][:], xw[:].indirect(offsets[:, 8 * c : 8 * c + 8]))
+
+        w23_bf = sb.tile([P, 2, N, 4], BF16, name="w23_bf", align_bytes=64)
+        w23_q = sb.tile([P, 2 * N], U32, name="w23_q", align_bytes=64)
+        w23_s = sb.tile([P, 2 * N], U8, name="w23_s", align_bytes=64)
+        nc.scalar.activation(
+            w23_bf[:, 0].rearrange("p (c i) j -> p c j i", i=4), w23_raw[:, 0].rearrange("p j (c i) -> p c j i", i=4), COPY
+        )
+        nc.vector.tensor_copy(
+            w23_bf[:, 1].rearrange("p (c i) j -> p c j i", i=4), w23_raw[:, 1].rearrange("p j (c i) -> p c j i", i=4)
+        )
+        nc.vector.quantize_mx(out=w23_q[:].bitcast(FP8X4), scales=w23_s[:], in_=w23_bf[:].rearrange("p w n j -> p (w n j)"))
+
+        hb = [sb.tile([P, 2, 128, 4], BF16, name=f"hb{u}", align_bytes=64) for u in range(2)]
+        zb = [sb.tile([P, 128, 4], BF16, name=f"zb{u}", align_bytes=64) for u in range(2)]
+        hq = [sb.tile([P, 256], U32, name=f"hq{u}", align_bytes=64) for u in range(2)]
+        hs = [sb.tile([P, 256], U8, name=f"hs{u}", align_bytes=64) for u in range(2)]
+        zq = [sb.tile([P, 128], U32, name=f"zq{u}", align_bytes=64) for u in range(2)]
+        zs = [sb.tile([P, 128], U8, name=f"zs{u}", align_bytes=64) for u in range(2)]
+
+        def layer1(c):
+            bank = ps.tile([P, 4, CH], F32, name=f"h_bank{c}")
+            for t in range(4):
+                nc.tensor.matmul_mx(
+                    out=bank[:, t, :],
+                    lhsT=w1_q[:, 128 * t : 128 * t + 128].bitcast(FP8X4),
+                    lhsT_scale=w1_s[:, 128 * t : 128 * t + 128],
+                    rhs=gw[c][:].bitcast(FP8X4),
+                    rhs_scale=gs[:, CH * c : CH * c + CH],
+                    start=True,
+                    stop=True,
+                )
+            u, v0 = c // 2, 64 * (c % 2)
+            nc.scalar.activation(hb[u][:, :, v0 : v0 + 64, :], bank[:].rearrange("p t (v d) -> p d v t", d=2), RELU)
+
+        def requantise(c):
+            u, v0 = c // 2, 64 * (c % 2)
+            vs = slice(v0, v0 + 64)
+            nc.vector.tensor_tensor(zb[u][:, vs, :], hb[u][:, 0, vs, :], hb[u][:, 1, vs, :], MAX)
+            for d in range(2):
+                cols = slice(128 * d + v0, 128 * d + v0 + 64)
+                nc.vector.quantize_mx(
+                    out=hq[u][:, cols].bitcast(FP8X4), scales=hs[u][:, cols], in_=hb[u][:, d, vs, :].rearrange("p v t -> p (v t)")
+                )
+            nc.vector.quantize_mx(
+                out=zq[u][:, vs].bitcast(FP8X4), scales=zs[u][:, vs], in_=zb[u][:, vs, :].rearrange("p v t -> p (v t)")
+            )
+
+        def layer2(u):
+            bank = ps.tile([P, 2, 128], F32, name=f"o_bank{u}")
+            nc.tensor.matmul_mx(
+                out=bank[:].rearrange("p d v -> p (d v)"),
+                lhsT=w23_q[:, 0:N].bitcast(FP8X4),
+                lhsT_scale=w23_s[:, 0:N],
+                rhs=hq[u][:].bitcast(FP8X4),
+                rhs_scale=hs[u][:],
+                start=True,
+                stop=False,
+            )
+            for d in range(2):
+                nc.tensor.matmul_mx(
+                    out=bank[:, d, :],
+                    lhsT=w23_q[:, N : 2 * N].bitcast(FP8X4),
+                    lhsT_scale=w23_s[:, N : 2 * N],
+                    rhs=zq[u][:].bitcast(FP8X4),
+                    rhs_scale=zs[u][:],
+                    start=False,
+                    stop=(d == 1),
+                )
+            res = sb.tile([P, 128, 2], F32, name=f"res{u}", align_bytes=64)
+            nc.scalar.activation(res[:], bank[:].rearrange("p d v -> p v d"), COPY)
+            nc.sync.dma_start(out=out[:, 256 * u : 256 * u + 256], in_=res[:].rearrange("p v d -> p (v d)"))
+
+        for c in range(4):
+            layer1(c)
+        for c in range(4):
+            requantise(c)
+            if c % 2 == 1:
+                layer2(c // 2)

@@ -18,73 +18,70 @@ MAX = mybir.AluOpType.max
 
 P = 128
 CH = 128
-W1_SPLIT = 44
+W1_SPLIT = 40
 
 
 def tile_picked_ypnseg_max_p_kernel(tc, x_words, x_scales, w1, w2, w3, offs, out):
     nc = tc.nc
     with ExitStack() as ctx:
         sb = ctx.enter_context(tc.tile_pool(name="sb", bufs=1))
-        reuse = ctx.enter_context(tc.tile_pool(name="reuse", bufs=1))
         ps = ctx.enter_context(tc.psum_pool(name="ps", bufs=1))
 
         offsets = sb.tile([P, S // 16], U16, name="offsets")
         xw = sb.tile([P, T], U32, name="xw", align_bytes=64)
-        xs = reuse.tile([P, T], U8, name="xs", align_bytes=64, offset=0)
+        xs = sb.tile([P, T], U8, name="xs", align_bytes=64)
         w1_raw = [sb.tile([P, 4, H // 2], F32, name=f"w1_raw{h}", align_bytes=64) for h in range(2)]
+        w23_raw = [sb.tile([P, 4, N], F32, name=f"w23_raw{h}", align_bytes=64) for h in range(2)]
 
         w1_rows = w1.rearrange("(p j) c -> p j c", j=4)
         nc.vector.memset(xs[:].bitcast(I32), 0)
         nc.sync.dma_start(out=w1_raw[0][:], in_=w1_rows[:, :, 0 : H // 2])
         nc.sync.dma_start(offsets[:], offs)
         for q in range(4):
-            nc.scalar.dma_start(out=xs[32 * q : 32 * q + 4, :].bitcast(I32), in_=x_scales[0, 4 * q : 4 * q + 4, :].bitcast(I32))
+            nc.sync.dma_start(out=xs[32 * q : 32 * q + 4, :].bitcast(I32), in_=x_scales[0, 4 * q : 4 * q + 4, :].bitcast(I32))
         nc.sync.dma_start(out=w1_raw[1][:], in_=w1_rows[:, :, H // 2 : H])
         nc.sync.dma_start(out=xw[:].bitcast(I32), in_=x_words[0].rearrange("p n t -> p (n t)").bitcast(I32))
+        nc.sync.dma_start(out=w23_raw[0][:], in_=w2.rearrange("(p j) c -> p j c", j=4))
+        nc.sync.dma_start(out=w23_raw[1][:], in_=w3.rearrange("(p j) c -> p j c", j=4))
 
         gs = sb.tile([P, S], U8, name="gs", align_bytes=64)
         nc.vector.tensor_copy(gs[:], xs[:].indirect(offsets[:]))
 
-        w1_bf = [
-            sb.tile([P, 4, 64, 4], BF16, name="w1_bf0", align_bytes=64),
-            reuse.tile([P, 4, 64, 4], BF16, name="w1_bf1", align_bytes=64, offset=512),
-        ]
+        w1_bf = sb.tile([P, 4, 128, 4], BF16, name="w1_bf", align_bytes=64)
         w1_q = sb.tile([P, H], U32, name="w1_q", align_bytes=64)
-        w1_s = reuse.tile([P, H], U8, name="w1_s", align_bytes=64, offset=0)
+        w1_s = sb.tile([P, H], U8, name="w1_s", align_bytes=64)
 
         def w1_views(h, m0, m1):
-            dst = w1_bf[h][:].rearrange("p t m j -> p m t j")[:, m0:m1]
+            dst = w1_bf[:].rearrange("p t m j -> p m t j")[:, 64 * h + m0 : 64 * h + m1]
             src = w1_raw[h][:].rearrange("p j (m t) -> p m t j", t=4)[:, m0:m1]
             return dst, src
 
         dst, src = w1_views(0, 0, 64)
         nc.scalar.activation(dst, src, COPY)
-        w23_raw = sb.tile([P, 2, 4, N], F32, name="w1_raw0", align_bytes=64)
-        nc.sync.dma_start(out=w23_raw[:, 0], in_=w2.rearrange("(p j) c -> p j c", j=4))
-        nc.sync.dma_start(out=w23_raw[:, 1], in_=w3.rearrange("(p j) c -> p j c", j=4))
         dst, src = w1_views(1, 0, W1_SPLIT)
         nc.vector.tensor_copy(dst, src)
         dst, src = w1_views(1, W1_SPLIT, 64)
         nc.scalar.activation(dst, src, COPY)
-        for h in range(2):
-            for t in range(4):
-                cols = slice(128 * t + 64 * h, 128 * t + 64 * h + 64)
-                nc.vector.quantize_mx(
-                    out=w1_q[:, cols].bitcast(FP8X4), scales=w1_s[:, cols], in_=w1_bf[h][:, t].rearrange("p m j -> p (m j)")
-                )
 
         gw = [sb.tile([P, CH], U32, name=f"gw{c}", align_bytes=64) for c in range(4)]
         for c in range(4):
+            if c < 2:
+                cols = slice(256 * c, 256 * c + 256)
+                nc.vector.quantize_mx(
+                    out=w1_q[:, cols].bitcast(FP8X4),
+                    scales=w1_s[:, cols],
+                    in_=w1_bf[:, 2 * c : 2 * c + 2].rearrange("p t m j -> p (t m j)"),
+                )
             nc.vector.tensor_copy(gw[c][:], xw[:].indirect(offsets[:, 8 * c : 8 * c + 8]))
 
         w23_bf = sb.tile([P, 2, N, 4], BF16, name="w23_bf", align_bytes=64)
         w23_q = sb.tile([P, 2 * N], U32, name="w23_q", align_bytes=64)
         w23_s = sb.tile([P, 2 * N], U8, name="w23_s", align_bytes=64)
         nc.scalar.activation(
-            w23_bf[:, 0].rearrange("p (c i) j -> p c j i", i=4), w23_raw[:, 0].rearrange("p j (c i) -> p c j i", i=4), COPY
+            w23_bf[:, 0].rearrange("p (c i) j -> p c j i", i=4), w23_raw[0][:].rearrange("p j (c i) -> p c j i", i=4), COPY
         )
         nc.vector.tensor_copy(
-            w23_bf[:, 1].rearrange("p (c i) j -> p c j i", i=4), w23_raw[:, 1].rearrange("p j (c i) -> p c j i", i=4)
+            w23_bf[:, 1].rearrange("p (c i) j -> p c j i", i=4), w23_raw[1][:].rearrange("p j (c i) -> p c j i", i=4)
         )
         nc.vector.quantize_mx(out=w23_q[:].bitcast(FP8X4), scales=w23_s[:], in_=w23_bf[:].rearrange("p w n j -> p (w n j)"))
 
@@ -110,15 +107,17 @@ def tile_picked_ypnseg_max_p_kernel(tc, x_words, x_scales, w1, w2, w3, offs, out
             u, v0 = c // 2, 64 * (c % 2)
             nc.scalar.activation(hb[u][:, :, v0 : v0 + 64, :], bank[:].rearrange("p t (v d) -> p d v t", d=2), RELU)
 
-        def requantise(c):
-            u, v0 = c // 2, 64 * (c % 2)
-            vs = slice(v0, v0 + 64)
+        def requantise(u, v0, v1):
+            vs = slice(v0, v1)
             nc.vector.tensor_tensor(zb[u][:, vs, :], hb[u][:, 0, vs, :], hb[u][:, 1, vs, :], MAX)
-            for d in range(2):
-                cols = slice(128 * d + v0, 128 * d + v0 + 64)
-                nc.vector.quantize_mx(
-                    out=hq[u][:, cols].bitcast(FP8X4), scales=hs[u][:, cols], in_=hb[u][:, d, vs, :].rearrange("p v t -> p (v t)")
-                )
+            if v1 - v0 == 128:
+                nc.vector.quantize_mx(out=hq[u][:].bitcast(FP8X4), scales=hs[u][:], in_=hb[u][:].rearrange("p d v t -> p (d v t)"))
+            else:
+                for d in range(2):
+                    cols = slice(128 * d + v0, 128 * d + v1)
+                    nc.vector.quantize_mx(
+                        out=hq[u][:, cols].bitcast(FP8X4), scales=hs[u][:, cols], in_=hb[u][:, d, vs, :].rearrange("p v t -> p (v t)")
+                    )
             nc.vector.quantize_mx(
                 out=zq[u][:, vs].bitcast(FP8X4), scales=zs[u][:, vs], in_=zb[u][:, vs, :].rearrange("p v t -> p (v t)")
             )
@@ -150,7 +149,8 @@ def tile_picked_ypnseg_max_p_kernel(tc, x_words, x_scales, w1, w2, w3, offs, out
 
         for c in range(4):
             layer1(c)
-        for c in range(4):
-            requantise(c)
-            if c % 2 == 1:
-                layer2(c // 2)
+        requantise(0, 0, 128)
+        layer2(0)
+        requantise(1, 0, 64)
+        requantise(1, 64, 128)
+        layer2(1)

@@ -15,10 +15,11 @@ FP8X4 = mybir.dt.float8_e4m3fn_x4
 COPY = mybir.ActivationFunctionType.Copy
 RELU = mybir.ActivationFunctionType.Relu
 MAX = mybir.AluOpType.max
+ADD = mybir.AluOpType.add
 
 P = 128
 CH = 128
-W1_SPLIT = 40
+W1_SPLIT = 36
 
 
 def tile_picked_ypnseg_max_p_kernel(tc, x_words, x_scales, w1, w2, w3, offs, out):
@@ -63,15 +64,10 @@ def tile_picked_ypnseg_max_p_kernel(tc, x_words, x_scales, w1, w2, w3, offs, out
         dst, src = w1_views(1, W1_SPLIT, 64)
         nc.scalar.activation(dst, src, COPY)
 
+        nc.vector.quantize_mx(out=w1_q[:].bitcast(FP8X4), scales=w1_s[:], in_=w1_bf[:].rearrange("p t m j -> p (t m j)"))
+
         gw = [sb.tile([P, CH], U32, name=f"gw{c}", align_bytes=64) for c in range(4)]
         for c in range(4):
-            if c < 2:
-                cols = slice(256 * c, 256 * c + 256)
-                nc.vector.quantize_mx(
-                    out=w1_q[:, cols].bitcast(FP8X4),
-                    scales=w1_s[:, cols],
-                    in_=w1_bf[:, 2 * c : 2 * c + 2].rearrange("p t m j -> p (t m j)"),
-                )
             nc.vector.tensor_copy(gw[c][:], xw[:].indirect(offsets[:, 8 * c : 8 * c + 8]))
 
         w23_bf = sb.tile([P, 2, N, 4], BF16, name="w23_bf", align_bytes=64)
@@ -85,14 +81,16 @@ def tile_picked_ypnseg_max_p_kernel(tc, x_words, x_scales, w1, w2, w3, offs, out
         )
         nc.vector.quantize_mx(out=w23_q[:].bitcast(FP8X4), scales=w23_s[:], in_=w23_bf[:].rearrange("p w n j -> p (w n j)"))
 
-        hb = [sb.tile([P, 2, 128, 4], BF16, name=f"hb{u}", align_bytes=64) for u in range(2)]
-        zb = [sb.tile([P, 128, 4], BF16, name=f"zb{u}", align_bytes=64) for u in range(2)]
-        hq = [sb.tile([P, 256], U32, name=f"hq{u}", align_bytes=64) for u in range(2)]
-        hs = [sb.tile([P, 256], U8, name=f"hs{u}", align_bytes=64) for u in range(2)]
-        zq = [sb.tile([P, 128], U32, name=f"zq{u}", align_bytes=64) for u in range(2)]
-        zs = [sb.tile([P, 128], U8, name=f"zs{u}", align_bytes=64) for u in range(2)]
+        units = [(0, 256), (256, 128), (384, 128)]
+        hb = [sb.tile([P, 2, n // 2, 4], BF16, name=f"hb{u}", align_bytes=64) for u, (j0, n) in enumerate(units)]
+        zb = [sb.tile([P, n // 2, 4], BF16, name=f"zb{u}", align_bytes=64) for u, (j0, n) in enumerate(units)]
+        hq = [sb.tile([P, n], U32, name=f"hq{u}", align_bytes=64) for u, (j0, n) in enumerate(units)]
+        hs = [sb.tile([P, n], U8, name=f"hs{u}", align_bytes=64) for u, (j0, n) in enumerate(units)]
+        zq = [sb.tile([P, n // 2], U32, name=f"zq{u}", align_bytes=64) for u, (j0, n) in enumerate(units)]
+        zs = [sb.tile([P, n // 2], U8, name=f"zs{u}", align_bytes=64) for u, (j0, n) in enumerate(units)]
+        res = [sb.tile([P, n // 2, 2], F32, name=f"res{u}", align_bytes=64) for u, (j0, n) in enumerate(units)]
 
-        def layer1(c):
+        def layer1(c, u, v0):
             bank = ps.tile([P, 4, CH], F32, name=f"h_bank{c}")
             for t in range(4):
                 nc.tensor.matmul_mx(
@@ -104,53 +102,53 @@ def tile_picked_ypnseg_max_p_kernel(tc, x_words, x_scales, w1, w2, w3, offs, out
                     start=True,
                     stop=True,
                 )
-            u, v0 = c // 2, 64 * (c % 2)
             nc.scalar.activation(hb[u][:, :, v0 : v0 + 64, :], bank[:].rearrange("p t (v d) -> p d v t", d=2), RELU)
 
-        def requantise(u, v0, v1):
-            vs = slice(v0, v1)
-            nc.vector.tensor_tensor(zb[u][:, vs, :], hb[u][:, 0, vs, :], hb[u][:, 1, vs, :], MAX)
-            if v1 - v0 == 128:
-                nc.vector.quantize_mx(out=hq[u][:].bitcast(FP8X4), scales=hs[u][:], in_=hb[u][:].rearrange("p d v t -> p (d v t)"))
-            else:
-                for d in range(2):
-                    cols = slice(128 * d + v0, 128 * d + v1)
-                    nc.vector.quantize_mx(
-                        out=hq[u][:, cols].bitcast(FP8X4), scales=hs[u][:, cols], in_=hb[u][:, d, vs, :].rearrange("p v t -> p (v t)")
-                    )
-            nc.vector.quantize_mx(
-                out=zq[u][:, vs].bitcast(FP8X4), scales=zs[u][:, vs], in_=zb[u][:, vs, :].rearrange("p v t -> p (v t)")
-            )
+        def requantise(u):
+            nc.vector.tensor_tensor(zb[u][:], hb[u][:, 0], hb[u][:, 1], MAX)
+            nc.vector.quantize_mx(out=hq[u][:].bitcast(FP8X4), scales=hs[u][:], in_=hb[u][:].rearrange("p d v t -> p (d v t)"))
+            nc.vector.quantize_mx(out=zq[u][:].bitcast(FP8X4), scales=zs[u][:], in_=zb[u][:].rearrange("p v t -> p (v t)"))
 
-        def layer2(u):
-            bank = ps.tile([P, 2, 128], F32, name=f"o_bank{u}")
+        def project(dst, w, codes, scales, start, stop):
             nc.tensor.matmul_mx(
-                out=bank[:].rearrange("p d v -> p (d v)"),
-                lhsT=w23_q[:, 0:N].bitcast(FP8X4),
-                lhsT_scale=w23_s[:, 0:N],
-                rhs=hq[u][:].bitcast(FP8X4),
-                rhs_scale=hs[u][:],
-                start=True,
-                stop=False,
+                out=dst,
+                lhsT=w23_q[:, w * N : w * N + N].bitcast(FP8X4),
+                lhsT_scale=w23_s[:, w * N : w * N + N],
+                rhs=codes[:].bitcast(FP8X4),
+                rhs_scale=scales[:],
+                start=start,
+                stop=stop,
             )
-            for d in range(2):
-                nc.tensor.matmul_mx(
-                    out=bank[:, d, :],
-                    lhsT=w23_q[:, N : 2 * N].bitcast(FP8X4),
-                    lhsT_scale=w23_s[:, N : 2 * N],
-                    rhs=zq[u][:].bitcast(FP8X4),
-                    rhs_scale=zs[u][:],
-                    start=False,
-                    stop=(d == 1),
-                )
-            res = sb.tile([P, 128, 2], F32, name=f"res{u}", align_bytes=64)
-            nc.scalar.activation(res[:], bank[:].rearrange("p d v -> p v d"), COPY)
-            nc.sync.dma_start(out=out[:, 256 * u : 256 * u + 256], in_=res[:].rearrange("p v d -> p (v d)"))
 
-        for c in range(4):
-            layer1(c)
-        requantise(0, 0, 128)
-        layer2(0)
-        requantise(1, 0, 64)
-        requantise(1, 64, 128)
-        layer2(1)
+        def store(u):
+            j0, n = units[u]
+            nc.sync.dma_start(out=out[:, j0 : j0 + n], in_=res[u][:].rearrange("p v d -> p (v d)"))
+
+        def layer2_in_psum(u):
+            bank = ps.tile([P, 2, 128], F32, name="o_bank")
+            project(bank[:].rearrange("p d v -> p (d v)"), 0, hq[u], hs[u], True, False)
+            for d in range(2):
+                project(bank[:, d, :], 1, zq[u], zs[u], False, d == 1)
+            nc.scalar.activation(res[u][:], bank[:].rearrange("p d v -> p v d"), COPY)
+            store(u)
+
+        def layer2_short(u):
+            y_bank = ps.tile([P, 2, 64], F32, name=f"h_bank{u - 1}")
+            g_bank = ps.tile([P, 64], F32, name=f"g_bank{u}")
+            y_sb = sb.tile([P, 64, 2], F32, name=f"y_sb{u}", align_bytes=64)
+            project(y_bank[:].rearrange("p d v -> p (d v)"), 0, hq[u], hs[u], True, True)
+            project(g_bank[:], 1, zq[u], zs[u], True, True)
+            nc.scalar.activation(y_sb[:], y_bank[:].rearrange("p d v -> p v d"), COPY)
+            nc.vector.tensor_tensor(res[u][:], g_bank[:].unsqueeze(2).to_broadcast([P, 64, 2]), y_sb[:], ADD)
+            store(u)
+
+        layer1(0, 0, 0)
+        layer1(1, 0, 64)
+        layer1(2, 1, 0)
+        layer1(3, 2, 0)
+        requantise(0)
+        layer2_in_psum(0)
+        requantise(1)
+        requantise(2)
+        layer2_short(1)
+        layer2_short(2)

@@ -15,7 +15,6 @@ FP8X4 = mybir.dt.float8_e4m3fn_x4
 COPY = mybir.ActivationFunctionType.Copy
 RELU = mybir.ActivationFunctionType.Relu
 MAX = mybir.AluOpType.max
-ADD = mybir.AluOpType.add
 
 P = 128
 CH = 128
@@ -39,7 +38,7 @@ def tile_picked_ypnseg_max_p_kernel(tc, x_words, x_scales, w1, w2, w3, offs, out
         nc.sync.dma_start(out=w1_raw[0][:], in_=w1_rows[:, :, 0 : H // 2])
         nc.sync.dma_start(offsets[:], offs)
         for q in range(4):
-            nc.sync.dma_start(out=xs[32 * q : 32 * q + 4, :].bitcast(I32), in_=x_scales[0, 4 * q : 4 * q + 4, :].bitcast(I32))
+            nc.sync.dma_start(out=xs[q:128:32, :].bitcast(I32), in_=x_scales[0, q:16:4, :].bitcast(I32))
         nc.sync.dma_start(out=w1_raw[1][:], in_=w1_rows[:, :, H // 2 : H])
         nc.sync.dma_start(out=xw[:].bitcast(I32), in_=x_words[0].rearrange("p n t -> p (n t)").bitcast(I32))
         nc.sync.dma_start(out=w23_raw[0][:], in_=w2.rearrange("(p j) c -> p j c", j=4))
@@ -82,12 +81,21 @@ def tile_picked_ypnseg_max_p_kernel(tc, x_words, x_scales, w1, w2, w3, offs, out
         nc.vector.quantize_mx(out=w23_q[:].bitcast(FP8X4), scales=w23_s[:], in_=w23_bf[:].rearrange("p w n j -> p (w n j)"))
 
         units = [(0, 256), (256, 128), (384, 128)]
-        hb = [sb.tile([P, 2, n // 2, 4], BF16, name=f"hb{u}", align_bytes=64) for u, (j0, n) in enumerate(units)]
-        zb = [sb.tile([P, n // 2, 4], BF16, name=f"zb{u}", align_bytes=64) for u, (j0, n) in enumerate(units)]
-        hq = [sb.tile([P, n], U32, name=f"hq{u}", align_bytes=64) for u, (j0, n) in enumerate(units)]
-        hs = [sb.tile([P, n], U8, name=f"hs{u}", align_bytes=64) for u, (j0, n) in enumerate(units)]
-        zq = [sb.tile([P, n // 2], U32, name=f"zq{u}", align_bytes=64) for u, (j0, n) in enumerate(units)]
-        zs = [sb.tile([P, n // 2], U8, name=f"zs{u}", align_bytes=64) for u, (j0, n) in enumerate(units)]
+        first_h = sb.tile([P, 2, 128, 4], BF16, name="first_h", align_bytes=64)
+        mixed = sb.tile([P, 2, 128, 4], BF16, name="mixed", align_bytes=64)
+        last_h = sb.tile([P, 2, 64, 4], BF16, name="last_h", align_bytes=64)
+        hb = [first_h[:], mixed[:, 0].rearrange("p (d v) t -> p d v t", d=2), last_h[:]]
+        zb = [mixed[:, 1]] + [sb.tile([P, 64, 4], BF16, name=f"zb{u}", align_bytes=64)[:] for u in (1, 2)]
+        first_q = sb.tile([P, 256], U32, name="first_q", align_bytes=64)
+        first_s = sb.tile([P, 256], U8, name="first_s", align_bytes=64)
+        mixed_q = sb.tile([P, 256], U32, name="mixed_q", align_bytes=64)
+        mixed_s = sb.tile([P, 256], U8, name="mixed_s", align_bytes=64)
+        last_q = sb.tile([P, 128], U32, name="last_q", align_bytes=64)
+        last_s = sb.tile([P, 128], U8, name="last_s", align_bytes=64)
+        hq = [first_q[:], mixed_q[:, 0:128], last_q[:]]
+        hs = [first_s[:], mixed_s[:, 0:128], last_s[:]]
+        zq = [mixed_q[:, 128:256]] + [sb.tile([P, 128], U32, name=f"zq{u}", align_bytes=64)[:] for u in (1, 2)]
+        zs = [mixed_s[:, 128:256]] + [sb.tile([P, 128], U8, name=f"zs{u}", align_bytes=64)[:] for u in (1, 2)]
         res = [sb.tile([P, n // 2, 2], F32, name=f"res{u}", align_bytes=64) for u, (j0, n) in enumerate(units)]
 
         def layer1(c, u, v0):
@@ -104,18 +112,20 @@ def tile_picked_ypnseg_max_p_kernel(tc, x_words, x_scales, w1, w2, w3, offs, out
                 )
             nc.scalar.activation(hb[u][:, :, v0 : v0 + 64, :], bank[:].rearrange("p t (v d) -> p d v t", d=2), RELU)
 
-        def requantise(u):
-            nc.vector.tensor_tensor(zb[u][:], hb[u][:, 0], hb[u][:, 1], MAX)
-            nc.vector.quantize_mx(out=hq[u][:].bitcast(FP8X4), scales=hs[u][:], in_=hb[u][:].rearrange("p d v t -> p (d v t)"))
-            nc.vector.quantize_mx(out=zq[u][:].bitcast(FP8X4), scales=zs[u][:], in_=zb[u][:].rearrange("p v t -> p (v t)"))
+        def quantise(codes, scales, values):
+            nc.vector.quantize_mx(out=codes.bitcast(FP8X4), scales=scales, in_=values)
+
+        def pool(u, v0):
+            v = slice(v0, v0 + 64)
+            nc.vector.tensor_tensor(zb[u][:, v], hb[u][:, 0, v], hb[u][:, 1, v], MAX)
 
         def project(dst, w, codes, scales, start, stop):
             nc.tensor.matmul_mx(
                 out=dst,
                 lhsT=w23_q[:, w * N : w * N + N].bitcast(FP8X4),
                 lhsT_scale=w23_s[:, w * N : w * N + N],
-                rhs=codes[:].bitcast(FP8X4),
-                rhs_scale=scales[:],
+                rhs=codes.bitcast(FP8X4),
+                rhs_scale=scales,
                 start=start,
                 stop=stop,
             )
@@ -133,22 +143,33 @@ def tile_picked_ypnseg_max_p_kernel(tc, x_words, x_scales, w1, w2, w3, offs, out
             store(u)
 
         def layer2_short(u):
-            y_bank = ps.tile([P, 2, 64], F32, name=f"h_bank{u - 1}")
-            g_bank = ps.tile([P, 64], F32, name=f"g_bank{u}")
-            y_sb = sb.tile([P, 64, 2], F32, name=f"y_sb{u}", align_bytes=64)
-            project(y_bank[:].rearrange("p d v -> p (d v)"), 0, hq[u], hs[u], True, True)
-            project(g_bank[:], 1, zq[u], zs[u], True, True)
-            nc.scalar.activation(y_sb[:], y_bank[:].rearrange("p d v -> p v d"), COPY)
-            nc.vector.tensor_tensor(res[u][:], g_bank[:].unsqueeze(2).to_broadcast([P, 64, 2]), y_sb[:], ADD)
+            bank = ps.tile([P, 2, 64], F32, name=f"o_bank{u}")
+            project(bank[:].rearrange("p d v -> p (d v)"), 0, hq[u], hs[u], True, False)
+            project(bank[:].rearrange("p d v -> p (d v)"), 1, zq[u], zs[u], False, True)
+            if u == 2:
+                nc.vector.tensor_copy(res[u][:], bank[:].rearrange("p d v -> p v d"))
+            else:
+                nc.scalar.activation(res[u][:], bank[:].rearrange("p d v -> p v d"), COPY)
             store(u)
+
+        def quantise_pooled(u):
+            for d in range(2):
+                cols = slice(64 * d, 64 * d + 64)
+                quantise(zq[u][:, cols], zs[u][:, cols], zb[u].rearrange("p v t -> p (v t)"))
 
         layer1(0, 0, 0)
         layer1(1, 0, 64)
         layer1(2, 1, 0)
         layer1(3, 2, 0)
-        requantise(0)
+        pool(0, 0)
+        pool(0, 64)
+        quantise(hq[0], hs[0], first_h[:].rearrange("p d v t -> p (d v t)"))
+        pool(1, 0)
+        quantise(mixed_q[:], mixed_s[:], mixed[:].rearrange("p a v t -> p (a v t)"))
+        quantise_pooled(1)
+        pool(2, 0)
+        quantise(hq[2], hs[2], last_h[:].rearrange("p d v t -> p (d v t)"))
+        quantise_pooled(2)
         layer2_in_psum(0)
-        requantise(1)
-        requantise(2)
         layer2_short(1)
         layer2_short(2)

@@ -18,7 +18,6 @@ MAX = mybir.AluOpType.max
 
 P = 128
 CH = 128
-W1_SPLIT = 36
 
 
 def tile_picked_ypnseg_max_p_kernel(tc, x_words, x_scales, w1, w2, w3, offs, out):
@@ -47,27 +46,36 @@ def tile_picked_ypnseg_max_p_kernel(tc, x_words, x_scales, w1, w2, w3, offs, out
         gs = sb.tile([P, S], U8, name="gs", align_bytes=64)
         nc.vector.tensor_copy(gs[:], xs[:].indirect(offsets[:]))
 
-        w1_bf = sb.tile([P, 4, 128, 4], BF16, name="w1_bf", align_bytes=64)
+        w1_bf = [sb.tile([P, 2, 128, 4], BF16, name=f"w1_bf{a}", align_bytes=64) for a in range(2)]
         w1_q = sb.tile([P, H], U32, name="w1_q", align_bytes=64)
         w1_s = sb.tile([P, H], U8, name="w1_s", align_bytes=64)
 
-        def w1_views(h, m0, m1):
-            dst = w1_bf[:].rearrange("p t m j -> p m t j")[:, 64 * h + m0 : 64 * h + m1]
-            src = w1_raw[h][:].rearrange("p j (m t) -> p m t j", t=4)[:, m0:m1]
+        def w1_views(h, a):
+            dst = w1_bf[a][:, :, 64 * h : 64 * h + 64].rearrange("p t m j -> p m t j")
+            src = w1_raw[h][:].rearrange("p j (m t) -> p m t j", t=4)[:, :, 2 * a : 2 * a + 2]
             return dst, src
 
-        dst, src = w1_views(0, 0, 64)
-        nc.scalar.activation(dst, src, COPY)
-        dst, src = w1_views(1, 0, W1_SPLIT)
-        nc.vector.tensor_copy(dst, src)
-        dst, src = w1_views(1, W1_SPLIT, 64)
-        nc.scalar.activation(dst, src, COPY)
+        def quantise_w1(a):
+            cols = slice(256 * a, 256 * a + 256)
+            nc.vector.quantize_mx(
+                out=w1_q[:, cols].bitcast(FP8X4), scales=w1_s[:, cols], in_=w1_bf[a][:].rearrange("p t m j -> p (t m j)")
+            )
 
-        nc.vector.quantize_mx(out=w1_q[:].bitcast(FP8X4), scales=w1_s[:], in_=w1_bf[:].rearrange("p t m j -> p (t m j)"))
+        nc.scalar.activation(*w1_views(0, 0), COPY)
+        nc.scalar.activation(*w1_views(0, 1), COPY)
+        nc.scalar.activation(*w1_views(1, 0), COPY)
+        nc.scalar.activation(*w1_views(1, 1), COPY)
 
         gw = [sb.tile([P, CH], U32, name=f"gw{c}", align_bytes=64) for c in range(4)]
-        for c in range(4):
+
+        def gather_words(c):
             nc.vector.tensor_copy(gw[c][:], xw[:].indirect(offsets[:, 8 * c : 8 * c + 8]))
+
+        quantise_w1(0)
+        gather_words(0)
+        quantise_w1(1)
+        for c in range(1, 4):
+            gather_words(c)
 
         w23_bf = sb.tile([P, 2, N, 4], BF16, name="w23_bf", align_bytes=64)
         w23_q = sb.tile([P, 2 * N], U32, name="w23_q", align_bytes=64)

@@ -51,8 +51,8 @@ def tile_picked_ypnseg_max_p_kernel(tc, x_words, x_scales, w1, w2, w3, offs, out
         w1_s = sb.tile([P, H], U8, name="w1_s", align_bytes=64)
 
         def w1_views(h, a):
-            dst = w1_bf[a][:, :, 64 * h : 64 * h + 64].rearrange("p t m j -> p m t j")
-            src = w1_raw[h][:].rearrange("p j (m t) -> p m t j", t=4)[:, :, 2 * a : 2 * a + 2]
+            dst = w1_bf[a][:, :, 64 * h : 64 * h + 64].rearrange("p t m j -> p m j t")
+            src = w1_raw[h][:].rearrange("p j (m t) -> p m j t", t=4)[:, :, :, 2 * a : 2 * a + 2]
             return dst, src
 
         def quantise_w1(a):

@@ -43,8 +43,29 @@ def tile_picked_ypnseg_max_p_kernel(tc, x_words, x_scales, w1, w2, w3, offs, out
         nc.sync.dma_start(out=w23_raw[0][:], in_=w2.rearrange("(p j) c -> p j c", j=4))
         nc.sync.dma_start(out=w23_raw[1][:], in_=w3.rearrange("(p j) c -> p j c", j=4))
 
-        gs = sb.tile([P, S], U8, name="gs", align_bytes=64)
-        nc.vector.tensor_copy(gs[:], xs[:].indirect(offsets[:]))
+        idle_values = sb.tile([P, 4 * S], BF16, name="idle_values", align_bytes=64)
+        idle_q = sb.tile([P, S], U32, name="idle_q", align_bytes=64)
+        idle_s = sb.tile([P, S], U8, name="idle_s", align_bytes=64)
+        nc.vector.memset(idle_values[:].bitcast(I32), 0)
+        nc.vector.quantize_mx(out=idle_q[:].bitcast(FP8X4), scales=idle_s[:], in_=idle_values[:])
+
+        gs_early = sb.tile([P, 3 * CH], U8, name="gs_early", align_bytes=64)
+        gs_late = sb.tile([P, CH], U8, name="gs_late", align_bytes=64)
+        nc.vector.tensor_copy(gs_early[:], xs[:].indirect(offsets[:, 0:24]))
+        nc.vector.tensor_copy(gs_late[:], xs[:].indirect(offsets[:, 24:32]))
+        gs = [gs_early[:, CH * c : CH * c + CH] for c in range(3)] + [gs_late[:]]
+
+        warm = ps.tile([32, S], F32, name="warm")
+        for turn in range(2):
+            nc.tensor.matmul_mx(
+                out=warm[:],
+                lhsT=idle_q[:, 0:32].bitcast(FP8X4),
+                lhsT_scale=gs_early[:, 0:32],
+                rhs=idle_q[:].bitcast(FP8X4),
+                rhs_scale=idle_s[:],
+                start=True,
+                stop=True,
+            )
 
         w1_bf = [sb.tile([P, 2, 128, 4], BF16, name=f"w1_bf{a}", align_bytes=64) for a in range(2)]
         w1_q = sb.tile([P, H], U32, name="w1_q", align_bytes=64)
@@ -114,7 +135,7 @@ def tile_picked_ypnseg_max_p_kernel(tc, x_words, x_scales, w1, w2, w3, offs, out
                     lhsT=w1_q[:, 128 * t : 128 * t + 128].bitcast(FP8X4),
                     lhsT_scale=w1_s[:, 128 * t : 128 * t + 128],
                     rhs=gw[c][:].bitcast(FP8X4),
-                    rhs_scale=gs[:, CH * c : CH * c + CH],
+                    rhs_scale=gs[c],
                     start=True,
                     stop=True,
                 )

@@ -49,18 +49,15 @@ def tile_picked_ypnseg_max_p_kernel(tc, x_words, x_scales, w1, w2, w3, offs, out
         nc.vector.memset(idle_values[:].bitcast(I32), 0)
         nc.vector.quantize_mx(out=idle_q[:].bitcast(FP8X4), scales=idle_s[:], in_=idle_values[:])
 
-        gs_early = sb.tile([P, 3 * CH], U8, name="gs_early", align_bytes=64)
-        gs_late = sb.tile([P, CH], U8, name="gs_late", align_bytes=64)
-        nc.vector.tensor_copy(gs_early[:], xs[:].indirect(offsets[:, 0:24]))
-        nc.vector.tensor_copy(gs_late[:], xs[:].indirect(offsets[:, 24:32]))
-        gs = [gs_early[:, CH * c : CH * c + CH] for c in range(3)] + [gs_late[:]]
+        gs = sb.tile([P, S], U8, name="gs", align_bytes=64)
+        nc.vector.tensor_copy(gs[:], xs[:].indirect(offsets[:]))
 
         warm = ps.tile([32, S], F32, name="warm")
         for turn in range(2):
             nc.tensor.matmul_mx(
                 out=warm[:],
                 lhsT=idle_q[:, 0:32].bitcast(FP8X4),
-                lhsT_scale=gs_early[:, 0:32],
+                lhsT_scale=gs[:, 0:32],
                 rhs=idle_q[:].bitcast(FP8X4),
                 rhs_scale=idle_s[:],
                 start=True,
@@ -135,7 +132,7 @@ def tile_picked_ypnseg_max_p_kernel(tc, x_words, x_scales, w1, w2, w3, offs, out
                     lhsT=w1_q[:, 128 * t : 128 * t + 128].bitcast(FP8X4),
                     lhsT_scale=w1_s[:, 128 * t : 128 * t + 128],
                     rhs=gw[c][:].bitcast(FP8X4),
-                    rhs_scale=gs[c],
+                    rhs_scale=gs[:, CH * c : CH * c + CH],
                     start=True,
                     stop=True,
                 )

@@ -96,15 +96,17 @@ def tile_picked_ypnseg_max_p_kernel(tc, x_words, x_scales, w1, w2, w3, offs, out
             gather_words(c)
 
         w23_bf = sb.tile([P, 2, N, 4], BF16, name="w23_bf", align_bytes=64)
-        w23_q = sb.tile([P, 2 * N], U32, name="w23_q", align_bytes=64)
-        w23_s = sb.tile([P, 2 * N], U8, name="w23_s", align_bytes=64)
+        row_q = sb.tile([P, 320 + 2 * N], U32, name="row_q", align_bytes=64)
+        row_s = sb.tile([P, 320 + 2 * N], U8, name="row_s", align_bytes=64)
+        w23_q = row_q[:, 320 : 320 + 2 * N]
+        w23_s = row_s[:, 320 : 320 + 2 * N]
         nc.scalar.activation(
             w23_bf[:, 0].rearrange("p (c i) j -> p c j i", i=4), w23_raw[0][:].rearrange("p j (c i) -> p c j i", i=4), COPY
         )
         nc.vector.tensor_copy(
             w23_bf[:, 1].rearrange("p (c i) j -> p c j i", i=4), w23_raw[1][:].rearrange("p j (c i) -> p c j i", i=4)
         )
-        nc.vector.quantize_mx(out=w23_q[:].bitcast(FP8X4), scales=w23_s[:], in_=w23_bf[:].rearrange("p w n j -> p (w n j)"))
+        nc.vector.quantize_mx(out=w23_q.bitcast(FP8X4), scales=w23_s, in_=w23_bf[:].rearrange("p w n j -> p (w n j)"))
 
         units = [(0, 256), (256, 128), (384, 128)]
         first_h = sb.tile([P, 2, 128, 4], BF16, name="first_h", align_bytes=64)
@@ -114,14 +116,14 @@ def tile_picked_ypnseg_max_p_kernel(tc, x_words, x_scales, w1, w2, w3, offs, out
         zb = [mixed[:, 1]] + [sb.tile([P, 64, 4], BF16, name=f"zb{u}", align_bytes=64)[:] for u in (1, 2)]
         first_q = sb.tile([P, 256], U32, name="first_q", align_bytes=64)
         first_s = sb.tile([P, 256], U8, name="first_s", align_bytes=64)
-        mixed_q = sb.tile([P, 256], U32, name="mixed_q", align_bytes=64)
-        mixed_s = sb.tile([P, 256], U8, name="mixed_s", align_bytes=64)
+        mixed_q = row_q[:, 0:256]
+        mixed_s = row_s[:, 0:256]
         last_q = sb.tile([P, 128], U32, name="last_q", align_bytes=64)
         last_s = sb.tile([P, 128], U8, name="last_s", align_bytes=64)
         hq = [first_q[:], mixed_q[:, 0:128], last_q[:]]
         hs = [first_s[:], mixed_s[:, 0:128], last_s[:]]
-        zq = [mixed_q[:, 128:256]] + [sb.tile([P, 128], U32, name=f"zq{u}", align_bytes=64)[:] for u in (1, 2)]
-        zs = [mixed_s[:, 128:256]] + [sb.tile([P, 128], U8, name=f"zs{u}", align_bytes=64)[:] for u in (1, 2)]
+        zq = [mixed_q[:, 128:256], row_q[:, 256:320], sb.tile([P, 128], U32, name="zq2", align_bytes=64)[:]]
+        zs = [mixed_s[:, 128:256], row_s[:, 256:320], sb.tile([P, 128], U8, name="zs2", align_bytes=64)[:]]
         res = [sb.tile([P, n // 2, 2], F32, name=f"res{u}", align_bytes=64) for u, (j0, n) in enumerate(units)]
 
         def layer1(c, u, v0):
@@ -178,6 +180,14 @@ def tile_picked_ypnseg_max_p_kernel(tc, x_words, x_scales, w1, w2, w3, offs, out
                 nc.scalar.activation(res[u][:], bank[:].rearrange("p d v -> p v d"), COPY)
             store(u)
 
+        def layer2_padded(u):
+            bank = ps.tile([P, 256], F32, name="o_bank1")
+            project(bank[:, 0:128], 1, row_q[:, 192:320], row_s[:, 192:320], True, False)
+            project(bank[:, 128:256], 1, row_q[:, 256:384], row_s[:, 256:384], False, False)
+            project(bank[:, 64:192], 0, hq[u], hs[u], False, True)
+            nc.scalar.activation(res[u][:], bank[:, 64:192].rearrange("p (d v) -> p v d", d=2), COPY)
+            store(u)
+
         def quantise_pooled(u):
             for d in range(2):
                 cols = slice(64 * d, 64 * d + 64)
@@ -191,11 +201,11 @@ def tile_picked_ypnseg_max_p_kernel(tc, x_words, x_scales, w1, w2, w3, offs, out
         pool(0, 64)
         quantise(hq[0], hs[0], first_h[:].rearrange("p d v t -> p (d v t)"))
         pool(1, 0)
-        quantise(mixed_q[:], mixed_s[:], mixed[:].rearrange("p a v t -> p (a v t)"))
-        quantise_pooled(1)
+        quantise(mixed_q, mixed_s, mixed[:].rearrange("p a v t -> p (a v t)"))
+        quantise(zq[1], zs[1], zb[1].rearrange("p v t -> p (v t)"))
         pool(2, 0)
         quantise(hq[2], hs[2], last_h[:].rearrange("p d v t -> p (d v t)"))
         quantise_pooled(2)
         layer2_in_psum(0)
-        layer2_short(1)
+        layer2_padded(1)
         layer2_short(2)

@@ -17,7 +17,9 @@ RELU = mybir.ActivationFunctionType.Relu
 MAX = mybir.AluOpType.max
 
 P = 128
-CH = 128
+CHUNK = 128
+CLOUDS = CHUNK // 2
+ENTRIES = 16
 
 
 def tile_picked_ypnseg_max_p_kernel(tc, x_words, x_scales, w1, w2, w3, offs, out):
@@ -26,68 +28,48 @@ def tile_picked_ypnseg_max_p_kernel(tc, x_words, x_scales, w1, w2, w3, offs, out
         sb = ctx.enter_context(tc.tile_pool(name="sb", bufs=1))
         ps = ctx.enter_context(tc.psum_pool(name="ps", bufs=1))
 
-        offsets = sb.tile([P, S // 16], U16, name="offsets")
-        xw = sb.tile([P, T], U32, name="xw", align_bytes=64)
-        xs = sb.tile([P, T], U8, name="xs", align_bytes=64)
-        w1_raw = [sb.tile([P, 4, H // 2], F32, name=f"w1_raw{h}", align_bytes=64) for h in range(2)]
-        w23_raw = [sb.tile([P, 4, N], F32, name=f"w23_raw{h}", align_bytes=64) for h in range(2)]
+        offsets = sb.tile([P, S // ENTRIES], U16, name="offsets")
+        word_table = sb.tile([P, T], U32, name="word_table", align_bytes=64)
+        scale_table = sb.tile([P, T], U8, name="scale_table", align_bytes=64)
+        w1_raw = [sb.tile([P, 4, H // 2], F32, name=f"w1_raw{half}", align_bytes=64) for half in range(2)]
+        w23_raw = [sb.tile([P, 4, N], F32, name=f"w23_raw{w}", align_bytes=64) for w in range(2)]
 
         w1_rows = w1.rearrange("(p j) c -> p j c", j=4)
-        nc.vector.memset(xs[:].bitcast(I32), 0)
+        nc.vector.memset(scale_table[:].bitcast(I32), 0)
         nc.sync.dma_start(out=w1_raw[0][:], in_=w1_rows[:, :, 0 : H // 2])
         nc.sync.dma_start(offsets[:], offs)
-        for q in range(4):
-            nc.sync.dma_start(out=xs[q:128:32, :].bitcast(I32), in_=x_scales[0, q:16:4, :].bitcast(I32))
+        for r in range(4):
+            nc.sync.dma_start(out=scale_table[r:P:32, :].bitcast(I32), in_=x_scales[0, r:16:4, :].bitcast(I32))
         nc.sync.dma_start(out=w1_raw[1][:], in_=w1_rows[:, :, H // 2 : H])
-        nc.sync.dma_start(out=xw[:].bitcast(I32), in_=x_words[0].rearrange("p n t -> p (n t)").bitcast(I32))
+        nc.sync.dma_start(out=word_table[:].bitcast(I32), in_=x_words[0].rearrange("p n t -> p (n t)").bitcast(I32))
         nc.sync.dma_start(out=w23_raw[0][:], in_=w2.rearrange("(p j) c -> p j c", j=4))
         nc.sync.dma_start(out=w23_raw[1][:], in_=w3.rearrange("(p j) c -> p j c", j=4))
 
-        idle_values = sb.tile([P, 4 * S], BF16, name="idle_values", align_bytes=64)
-        idle_q = sb.tile([P, S], U32, name="idle_q", align_bytes=64)
-        idle_s = sb.tile([P, S], U8, name="idle_s", align_bytes=64)
-        nc.vector.memset(idle_values[:].bitcast(I32), 0)
-        nc.vector.quantize_mx(out=idle_q[:].bitcast(FP8X4), scales=idle_s[:], in_=idle_values[:])
+        x_scale = sb.tile([P, S], U8, name="x_scale", align_bytes=64)
+        nc.vector.tensor_copy(x_scale[:], scale_table[:].indirect(offsets[:]))
 
-        gs = sb.tile([P, S], U8, name="gs", align_bytes=64)
-        nc.vector.tensor_copy(gs[:], xs[:].indirect(offsets[:]))
+        w1_bf = [sb.tile([P, 2, P, 4], BF16, name=f"w1_bf{pair}", align_bytes=64) for pair in range(2)]
+        w1_code = sb.tile([P, H], U32, name="w1_code", align_bytes=64)
+        w1_scale = sb.tile([P, H], U8, name="w1_scale", align_bytes=64)
 
-        warm = ps.tile([32, S], F32, name="warm")
-        for turn in range(2):
-            nc.tensor.matmul_mx(
-                out=warm[:],
-                lhsT=idle_q[:, 0:32].bitcast(FP8X4),
-                lhsT_scale=gs[:, 0:32],
-                rhs=idle_q[:].bitcast(FP8X4),
-                rhs_scale=idle_s[:],
-                start=True,
-                stop=True,
-            )
+        def quantise(codes, scales, values):
+            nc.vector.quantize_mx(out=codes.bitcast(FP8X4), scales=scales, in_=values)
 
-        w1_bf = [sb.tile([P, 2, 128, 4], BF16, name=f"w1_bf{a}", align_bytes=64) for a in range(2)]
-        w1_q = sb.tile([P, H], U32, name="w1_q", align_bytes=64)
-        w1_s = sb.tile([P, H], U8, name="w1_s", align_bytes=64)
+        def quantise_w1(pair):
+            cols = slice(2 * P * pair, 2 * P * (pair + 1))
+            quantise(w1_code[:, cols], w1_scale[:, cols], w1_bf[pair][:].rearrange("p t m j -> p (t m j)"))
 
-        def w1_views(h, a):
-            dst = w1_bf[a][:, :, 64 * h : 64 * h + 64].rearrange("p t m j -> p m j t")
-            src = w1_raw[h][:].rearrange("p j (m t) -> p m j t", t=4)[:, :, :, 2 * a : 2 * a + 2]
-            return dst, src
+        for half in range(2):
+            for pair in range(2):
+                rounded = w1_bf[pair][:, :, P // 2 * half : P // 2 * (half + 1)].rearrange("p t m j -> p m j t")
+                loaded = w1_raw[half][:].rearrange("p j (m t) -> p m j t", t=4)[:, :, :, 2 * pair : 2 * pair + 2]
+                nc.scalar.activation(rounded, loaded, COPY)
 
-        def quantise_w1(a):
-            cols = slice(256 * a, 256 * a + 256)
-            nc.vector.quantize_mx(
-                out=w1_q[:, cols].bitcast(FP8X4), scales=w1_s[:, cols], in_=w1_bf[a][:].rearrange("p t m j -> p (t m j)")
-            )
-
-        nc.scalar.activation(*w1_views(0, 0), COPY)
-        nc.scalar.activation(*w1_views(0, 1), COPY)
-        nc.scalar.activation(*w1_views(1, 0), COPY)
-        nc.scalar.activation(*w1_views(1, 1), COPY)
-
-        gw = [sb.tile([P, CH], U32, name=f"gw{c}", align_bytes=64) for c in range(4)]
+        x_code = [sb.tile([P, CHUNK], U32, name=f"x_code{c}", align_bytes=64) for c in range(4)]
 
         def gather_words(c):
-            nc.vector.tensor_copy(gw[c][:], xw[:].indirect(offsets[:, 8 * c : 8 * c + 8]))
+            columns = CHUNK // ENTRIES
+            nc.vector.tensor_copy(x_code[c][:], word_table[:].indirect(offsets[:, columns * c : columns * (c + 1)]))
 
         quantise_w1(0)
         gather_words(0)
@@ -95,117 +77,113 @@ def tile_picked_ypnseg_max_p_kernel(tc, x_words, x_scales, w1, w2, w3, offs, out
         for c in range(1, 4):
             gather_words(c)
 
+        z_first_at = CHUNK
+        z_third_at = z_first_at + 2 * CLOUDS
+        w23_at = z_third_at + CLOUDS
         w23_bf = sb.tile([P, 2, N, 4], BF16, name="w23_bf", align_bytes=64)
-        row_q = sb.tile([P, 320 + 2 * N], U32, name="row_q", align_bytes=64)
-        row_s = sb.tile([P, 320 + 2 * N], U8, name="row_s", align_bytes=64)
-        w23_q = row_q[:, 320 : 320 + 2 * N]
-        w23_s = row_s[:, 320 : 320 + 2 * N]
-        nc.scalar.activation(
-            w23_bf[:, 0].rearrange("p (c i) j -> p c j i", i=4), w23_raw[0][:].rearrange("p j (c i) -> p c j i", i=4), COPY
-        )
-        nc.vector.tensor_copy(
-            w23_bf[:, 1].rearrange("p (c i) j -> p c j i", i=4), w23_raw[1][:].rearrange("p j (c i) -> p c j i", i=4)
-        )
-        nc.vector.quantize_mx(out=w23_q.bitcast(FP8X4), scales=w23_s, in_=w23_bf[:].rearrange("p w n j -> p (w n j)"))
+        row_code = sb.tile([P, w23_at + 2 * N], U32, name="row_code", align_bytes=64)
+        row_scale = sb.tile([P, w23_at + 2 * N], U8, name="row_scale", align_bytes=64)
 
-        units = [(0, 256), (256, 128), (384, 128)]
-        first_h = sb.tile([P, 2, 128, 4], BF16, name="first_h", align_bytes=64)
-        mixed = sb.tile([P, 2, 128, 4], BF16, name="mixed", align_bytes=64)
-        last_h = sb.tile([P, 2, 64, 4], BF16, name="last_h", align_bytes=64)
-        hb = [first_h[:], mixed[:, 0].rearrange("p (d v) t -> p d v t", d=2), last_h[:]]
-        zb = [mixed[:, 1]] + [sb.tile([P, 64, 4], BF16, name=f"zb{u}", align_bytes=64)[:] for u in (1, 2)]
-        first_q = sb.tile([P, 256], U32, name="first_q", align_bytes=64)
-        first_s = sb.tile([P, 256], U8, name="first_s", align_bytes=64)
-        mixed_q = row_q[:, 0:256]
-        mixed_s = row_s[:, 0:256]
-        last_q = sb.tile([P, 128], U32, name="last_q", align_bytes=64)
-        last_s = sb.tile([P, 128], U8, name="last_s", align_bytes=64)
-        hq = [first_q[:], mixed_q[:, 0:128], last_q[:]]
-        hs = [first_s[:], mixed_s[:, 0:128], last_s[:]]
-        zq = [mixed_q[:, 128:256], row_q[:, 256:320], sb.tile([P, 128], U32, name="zq2", align_bytes=64)[:]]
-        zs = [mixed_s[:, 128:256], row_s[:, 256:320], sb.tile([P, 128], U8, name="zs2", align_bytes=64)[:]]
-        res = [sb.tile([P, n // 2, 2], F32, name=f"res{u}", align_bytes=64) for u, (j0, n) in enumerate(units)]
+        def in_row(first, columns):
+            return row_code[:, first : first + columns], row_scale[:, first : first + columns]
 
-        def layer1(c, u, v0):
-            bank = ps.tile([P, 4, CH], F32, name=f"h_bank{c}")
+        def w23_views(w):
+            rounded = w23_bf[:, w].rearrange("p (c i) j -> p c j i", i=4)
+            return rounded, w23_raw[w][:].rearrange("p j (c i) -> p c j i", i=4)
+
+        nc.scalar.activation(*w23_views(0), COPY)
+        nc.vector.tensor_copy(*w23_views(1))
+        quantise(*in_row(w23_at, 2 * N), w23_bf[:].rearrange("p w n j -> p (w n j)"))
+
+        groups = [(0, 2 * CHUNK), (2 * CHUNK, CHUNK), (3 * CHUNK, CHUNK)]
+        h_first = sb.tile([P, 2, 2 * CLOUDS, 4], BF16, name="h_first", align_bytes=64)
+        h_third_z_first = sb.tile([P, 2, CHUNK, 4], BF16, name="h_third_z_first", align_bytes=64)
+        h_last = sb.tile([P, 2, CLOUDS, 4], BF16, name="h_last", align_bytes=64)
+        z_third = sb.tile([P, CLOUDS, 4], BF16, name="z_third", align_bytes=64)
+        z_last = sb.tile([P, CLOUDS, 4], BF16, name="z_last", align_bytes=64)
+        h_bf = [h_first[:], h_third_z_first[:, 0].rearrange("p (d v) t -> p d v t", d=2), h_last[:]]
+        z_bf = [h_third_z_first[:, 1], z_third[:], z_last[:]]
+        h_first_code = sb.tile([P, 2 * CHUNK], U32, name="h_first_code", align_bytes=64)
+        h_first_scale = sb.tile([P, 2 * CHUNK], U8, name="h_first_scale", align_bytes=64)
+        h_last_code = sb.tile([P, CHUNK], U32, name="h_last_code", align_bytes=64)
+        h_last_scale = sb.tile([P, CHUNK], U8, name="h_last_scale", align_bytes=64)
+        z_last_code = sb.tile([P, CHUNK], U32, name="z_last_code", align_bytes=64)
+        z_last_scale = sb.tile([P, CHUNK], U8, name="z_last_scale", align_bytes=64)
+        result = [sb.tile([P, n // 2, 2], F32, name=f"result{g}", align_bytes=64) for g, (j0, n) in enumerate(groups)]
+
+        def layer1(c, g, v0):
+            bank = ps.tile([P, 4, CHUNK], F32, name=f"h_bank{c}")
             for t in range(4):
                 nc.tensor.matmul_mx(
                     out=bank[:, t, :],
-                    lhsT=w1_q[:, 128 * t : 128 * t + 128].bitcast(FP8X4),
-                    lhsT_scale=w1_s[:, 128 * t : 128 * t + 128],
-                    rhs=gw[c][:].bitcast(FP8X4),
-                    rhs_scale=gs[:, CH * c : CH * c + CH],
+                    lhsT=w1_code[:, P * t : P * (t + 1)].bitcast(FP8X4),
+                    lhsT_scale=w1_scale[:, P * t : P * (t + 1)],
+                    rhs=x_code[c][:].bitcast(FP8X4),
+                    rhs_scale=x_scale[:, CHUNK * c : CHUNK * (c + 1)],
                     start=True,
                     stop=True,
                 )
-            nc.scalar.activation(hb[u][:, :, v0 : v0 + 64, :], bank[:].rearrange("p t (v d) -> p d v t", d=2), RELU)
+            nc.scalar.activation(h_bf[g][:, :, v0 : v0 + CLOUDS, :], bank[:].rearrange("p t (v d) -> p d v t", d=2), RELU)
 
-        def quantise(codes, scales, values):
-            nc.vector.quantize_mx(out=codes.bitcast(FP8X4), scales=scales, in_=values)
+        def pool(g, v0):
+            v = slice(v0, v0 + CLOUDS)
+            nc.vector.tensor_tensor(z_bf[g][:, v], h_bf[g][:, 0, v], h_bf[g][:, 1, v], MAX)
 
-        def pool(u, v0):
-            v = slice(v0, v0 + 64)
-            nc.vector.tensor_tensor(zb[u][:, v], hb[u][:, 0, v], hb[u][:, 1, v], MAX)
-
-        def project(dst, w, codes, scales, start, stop):
+        def project(sums, w, codes, scales, start, stop):
+            weight_code, weight_scale = in_row(w23_at + N * w, N)
             nc.tensor.matmul_mx(
-                out=dst,
-                lhsT=w23_q[:, w * N : w * N + N].bitcast(FP8X4),
-                lhsT_scale=w23_s[:, w * N : w * N + N],
+                out=sums,
+                lhsT=weight_code.bitcast(FP8X4),
+                lhsT_scale=weight_scale,
                 rhs=codes.bitcast(FP8X4),
                 rhs_scale=scales,
                 start=start,
                 stop=stop,
             )
 
-        def store(u):
-            j0, n = units[u]
-            nc.sync.dma_start(out=out[:, j0 : j0 + n], in_=res[u][:].rearrange("p v d -> p (v d)"))
+        def store(g):
+            j0, n = groups[g]
+            nc.sync.dma_start(out=out[:, j0 : j0 + n], in_=result[g][:].rearrange("p v d -> p (v d)"))
 
-        def layer2_in_psum(u):
-            bank = ps.tile([P, 2, 128], F32, name="o_bank")
-            project(bank[:].rearrange("p d v -> p (d v)"), 0, hq[u], hs[u], True, False)
+        def layer2_first():
+            bank = ps.tile([P, 2, 2 * CLOUDS], F32, name="out_bank0")
+            project(bank[:].rearrange("p d v -> p (d v)"), 0, h_first_code[:], h_first_scale[:], True, False)
             for d in range(2):
-                project(bank[:, d, :], 1, zq[u], zs[u], False, d == 1)
-            nc.scalar.activation(res[u][:], bank[:].rearrange("p d v -> p v d"), COPY)
-            store(u)
+                project(bank[:, d, :], 1, *in_row(z_first_at, 2 * CLOUDS), False, d == 1)
+            nc.scalar.activation(result[0][:], bank[:].rearrange("p d v -> p v d"), COPY)
+            store(0)
 
-        def layer2_short(u):
-            bank = ps.tile([P, 2, 64], F32, name=f"o_bank{u}")
-            project(bank[:].rearrange("p d v -> p (d v)"), 0, hq[u], hs[u], True, False)
-            project(bank[:].rearrange("p d v -> p (d v)"), 1, zq[u], zs[u], False, True)
-            if u == 2:
-                nc.vector.tensor_copy(res[u][:], bank[:].rearrange("p d v -> p v d"))
-            else:
-                nc.scalar.activation(res[u][:], bank[:].rearrange("p d v -> p v d"), COPY)
-            store(u)
+        def layer2_third():
+            bank = ps.tile([P, 2 * CHUNK], F32, name="out_bank1")
+            sums = bank[:, CLOUDS : CLOUDS + CHUNK]
+            project(bank[:, 0:CHUNK], 1, *in_row(z_third_at - CLOUDS, CHUNK), True, False)
+            project(bank[:, CHUNK : 2 * CHUNK], 1, *in_row(z_third_at, CHUNK), False, False)
+            project(sums, 0, *in_row(0, CHUNK), False, True)
+            nc.scalar.activation(result[1][:], sums.rearrange("p (d v) -> p v d", d=2), COPY)
+            store(1)
 
-        def layer2_padded(u):
-            bank = ps.tile([P, 256], F32, name="o_bank1")
-            project(bank[:, 0:128], 1, row_q[:, 192:320], row_s[:, 192:320], True, False)
-            project(bank[:, 128:256], 1, row_q[:, 256:384], row_s[:, 256:384], False, False)
-            project(bank[:, 64:192], 0, hq[u], hs[u], False, True)
-            nc.scalar.activation(res[u][:], bank[:, 64:192].rearrange("p (d v) -> p v d", d=2), COPY)
-            store(u)
-
-        def quantise_pooled(u):
-            for d in range(2):
-                cols = slice(64 * d, 64 * d + 64)
-                quantise(zq[u][:, cols], zs[u][:, cols], zb[u].rearrange("p v t -> p (v t)"))
+        def layer2_last():
+            bank = ps.tile([P, 2, CLOUDS], F32, name="out_bank2")
+            project(bank[:].rearrange("p d v -> p (d v)"), 0, h_last_code[:], h_last_scale[:], True, False)
+            project(bank[:].rearrange("p d v -> p (d v)"), 1, z_last_code[:], z_last_scale[:], False, True)
+            nc.vector.tensor_copy(result[2][:], bank[:].rearrange("p d v -> p v d"))
+            store(2)
 
         layer1(0, 0, 0)
-        layer1(1, 0, 64)
+        layer1(1, 0, CLOUDS)
         layer1(2, 1, 0)
         layer1(3, 2, 0)
         pool(0, 0)
-        pool(0, 64)
-        quantise(hq[0], hs[0], first_h[:].rearrange("p d v t -> p (d v t)"))
+        pool(0, CLOUDS)
+        quantise(h_first_code[:], h_first_scale[:], h_first[:].rearrange("p d v t -> p (d v t)"))
         pool(1, 0)
-        quantise(mixed_q, mixed_s, mixed[:].rearrange("p a v t -> p (a v t)"))
-        quantise(zq[1], zs[1], zb[1].rearrange("p v t -> p (v t)"))
+        quantise(*in_row(0, z_third_at), h_third_z_first[:].rearrange("p a v t -> p (a v t)"))
+        quantise(*in_row(z_third_at, CLOUDS), z_third[:].rearrange("p v t -> p (v t)"))
         pool(2, 0)
-        quantise(hq[2], hs[2], last_h[:].rearrange("p d v t -> p (d v t)"))
-        quantise_pooled(2)
-        layer2_in_psum(0)
-        layer2_padded(1)
-        layer2_short(2)
+        quantise(h_last_code[:], h_last_scale[:], h_last[:].rearrange("p d v t -> p (d v t)"))
+        for d in range(2):
+            cols = slice(CLOUDS * d, CLOUDS * (d + 1))
+            quantise(z_last_code[:, cols], z_last_scale[:, cols], z_last[:].rearrange("p v t -> p (v t)"))
+        layer2_first()
+        layer2_third()
+        layer2_last()

@@ -20,6 +20,10 @@ P = 128
 CHUNK = 128
 CLOUDS = CHUNK // 2
 ENTRIES = 16
+W2_SCALAR = 72
+W1_VECTOR = 20
+WARM_PASSES = 9
+WARM_ROWS = 32
 
 
 def tile_picked_ypnseg_max_p_kernel(tc, x_words, x_scales, w1, w2, w3, offs, out):
@@ -46,24 +50,47 @@ def tile_picked_ypnseg_max_p_kernel(tc, x_words, x_scales, w1, w2, w3, offs, out
         nc.sync.dma_start(out=w23_raw[1][:], in_=w3.rearrange("(p j) c -> p j c", j=4))
 
         x_scale = sb.tile([P, S], U8, name="x_scale", align_bytes=64)
-        nc.vector.tensor_copy(x_scale[:], scale_table[:].indirect(offsets[:]))
 
         w1_bf = [sb.tile([P, 2, P, 4], BF16, name=f"w1_bf{pair}", align_bytes=64) for pair in range(2)]
-        w1_code = sb.tile([P, H], U32, name="w1_code", align_bytes=64)
-        w1_scale = sb.tile([P, H], U8, name="w1_scale", align_bytes=64)
+        w1_at = [P // 2 + 2 * P, P // 2 + 3 * P, P // 2, P // 2 + P]
+        w1_code = sb.tile([P, P // 2 + H], U32, name="w1_code", align_bytes=64)
+        w1_scale = sb.tile([P, P // 2 + H], U8, name="w1_scale", align_bytes=64)
 
         def quantise(codes, scales, values):
             nc.vector.quantize_mx(out=codes.bitcast(FP8X4), scales=scales, in_=values)
 
-        def quantise_w1(pair):
-            cols = slice(2 * P * pair, 2 * P * (pair + 1))
-            quantise(w1_code[:, cols], w1_scale[:, cols], w1_bf[pair][:].rearrange("p t m j -> p (t m j)"))
+        def quantise_half(t, half, at):
+            cols = slice(at, at + P // 2)
+            values = w1_bf[t // 2][:, t % 2, P // 2 * half : P // 2 * (half + 1)].rearrange("p m j -> p (m j)")
+            quantise(w1_code[:, cols], w1_scale[:, cols], values)
 
-        for half in range(2):
-            for pair in range(2):
-                rounded = w1_bf[pair][:, :, P // 2 * half : P // 2 * (half + 1)].rearrange("p t m j -> p m j t")
-                loaded = w1_raw[half][:].rearrange("p j (m t) -> p m j t", t=4)[:, :, :, 2 * pair : 2 * pair + 2]
-                nc.scalar.activation(rounded, loaded, COPY)
+        def w1_views(half, pair, m0, m1):
+            rounded = w1_bf[pair][:, :, P // 2 * half + m0 : P // 2 * half + m1].rearrange("p t m j -> p m j t")
+            loaded = w1_raw[half][:].rearrange("p j (m t) -> p m j t", t=4)[:, m0:m1, :, 2 * pair : 2 * pair + 2]
+            return rounded, loaded
+
+        nc.vector.tensor_copy(*w1_views(0, 1, 0, P // 2))
+        nc.vector.tensor_copy(*w1_views(0, 0, 0, W1_VECTOR))
+        nc.scalar.activation(*w1_views(0, 0, W1_VECTOR, P // 2), COPY)
+
+        warm_bank = ps.tile([WARM_ROWS, 4, P], F32, name="warm_bank")
+        quantise_half(2, 0, w1_at[2])
+        quantise_half(2, 0, 0)
+        quantise_half(3, 0, w1_at[3])
+        for i in range(WARM_PASSES):
+            nc.tensor.matmul_mx(
+                out=warm_bank[:, i % 4, :],
+                lhsT=w1_code[:, 0:WARM_ROWS].bitcast(FP8X4),
+                lhsT_scale=w1_scale[:, 0:WARM_ROWS],
+                rhs=w1_code[:, 0:P].bitcast(FP8X4),
+                rhs_scale=w1_scale[:, 0:P],
+                start=True,
+                stop=True,
+            )
+        nc.vector.tensor_copy(x_scale[:], scale_table[:].indirect(offsets[:]))
+
+        for pair in range(2):
+            nc.scalar.activation(*w1_views(1, pair, 0, P // 2), COPY)
 
         x_code = [sb.tile([P, CHUNK], U32, name=f"x_code{c}", align_bytes=64) for c in range(4)]
 
@@ -71,9 +98,11 @@ def tile_picked_ypnseg_max_p_kernel(tc, x_words, x_scales, w1, w2, w3, offs, out
             columns = CHUNK // ENTRIES
             nc.vector.tensor_copy(x_code[c][:], word_table[:].indirect(offsets[:, columns * c : columns * (c + 1)]))
 
-        quantise_w1(0)
+        first_pair = slice(w1_at[0], w1_at[0] + 2 * P)
+        quantise(w1_code[:, first_pair], w1_scale[:, first_pair], w1_bf[0][:].rearrange("p t m j -> p (t m j)"))
         gather_words(0)
-        quantise_w1(1)
+        for t in range(2, 4):
+            quantise_half(t, 1, w1_at[t] + P // 2)
         for c in range(1, 4):
             gather_words(c)
 
@@ -87,12 +116,13 @@ def tile_picked_ypnseg_max_p_kernel(tc, x_words, x_scales, w1, w2, w3, offs, out
         def in_row(first, columns):
             return row_code[:, first : first + columns], row_scale[:, first : first + columns]
 
-        def w23_views(w):
-            rounded = w23_bf[:, w].rearrange("p (c i) j -> p c j i", i=4)
-            return rounded, w23_raw[w][:].rearrange("p j (c i) -> p c j i", i=4)
+        def w23_views(w, n0, n1):
+            rounded = w23_bf[:, w, n0:n1].rearrange("p (c i) j -> p c j i", i=4)
+            return rounded, w23_raw[w][:, :, n0:n1].rearrange("p j (c i) -> p c j i", i=4)
 
-        nc.scalar.activation(*w23_views(0), COPY)
-        nc.vector.tensor_copy(*w23_views(1))
+        nc.scalar.activation(*w23_views(0, 0, W2_SCALAR), COPY)
+        nc.vector.tensor_copy(*w23_views(0, W2_SCALAR, N))
+        nc.vector.tensor_copy(*w23_views(1, 0, N))
         quantise(*in_row(w23_at, 2 * N), w23_bf[:].rearrange("p w n j -> p (w n j)"))
 
         groups = [(0, 2 * CHUNK), (2 * CHUNK, CHUNK), (3 * CHUNK, CHUNK)]
@@ -116,8 +146,8 @@ def tile_picked_ypnseg_max_p_kernel(tc, x_words, x_scales, w1, w2, w3, offs, out
             for t in range(4):
                 nc.tensor.matmul_mx(
                     out=bank[:, t, :],
-                    lhsT=w1_code[:, P * t : P * (t + 1)].bitcast(FP8X4),
-                    lhsT_scale=w1_scale[:, P * t : P * (t + 1)],
+                    lhsT=w1_code[:, w1_at[t] : w1_at[t] + P].bitcast(FP8X4),
+                    lhsT_scale=w1_scale[:, w1_at[t] : w1_at[t] + P],
                     rhs=x_code[c][:].bitcast(FP8X4),
                     rhs_scale=x_scale[:, CHUNK * c : CHUNK * (c + 1)],
                     start=True,

@@ -75,12 +75,14 @@ def tile_picked_ypnseg_max_p_kernel(tc, x_words, x_scales, w1, w2, w3, offs, out
 
         warm_bank = ps.tile([WARM_ROWS, 4, P], F32, name="warm_bank")
         quantise_half(2, 0, w1_at[2])
-        quantise_half(2, 0, 0)
         quantise_half(3, 0, w1_at[3])
+        quantise_half(2, 0, 0)
+        warm_rows = sb.tile([P, WARM_ROWS], U32, name="warm_rows", align_bytes=64)
+        nc.scalar.copy(warm_rows[:], w1_code[:, 0:WARM_ROWS])
         for i in range(WARM_PASSES):
             nc.tensor.matmul_mx(
                 out=warm_bank[:, i % 4, :],
-                lhsT=w1_code[:, 0:WARM_ROWS].bitcast(FP8X4),
+                lhsT=warm_rows[:].bitcast(FP8X4),
                 lhsT_scale=w1_scale[:, 0:WARM_ROWS],
                 rhs=w1_code[:, 0:P].bitcast(FP8X4),
                 rhs_scale=w1_scale[:, 0:P],

@@ -208,8 +208,9 @@ def tile_picked_ypnseg_max_p_kernel(tc, x_words, x_scales, w1, w2, w3, offs, out
         pool(0, 0)
         pool(0, CLOUDS)
         quantise(h_first_code[:], h_first_scale[:], h_first[:].rearrange("p d v t -> p (d v t)"))
+        quantise(*in_row(z_first_at, 2 * CLOUDS), z_bf[0].rearrange("p v t -> p (v t)"))
         pool(1, 0)
-        quantise(*in_row(0, z_third_at), h_third_z_first[:].rearrange("p a v t -> p (a v t)"))
+        quantise(*in_row(0, CHUNK), h_bf[1].rearrange("p d v t -> p (d v t)"))
         quantise(*in_row(z_third_at, CLOUDS), z_third[:].rearrange("p v t -> p (v t)"))
         pool(2, 0)
         quantise(h_last_code[:], h_last_scale[:], h_last[:].rearrange("p d v t -> p (d v t)"))

@@ -75,14 +75,12 @@ def tile_picked_ypnseg_max_p_kernel(tc, x_words, x_scales, w1, w2, w3, offs, out
 
         warm_bank = ps.tile([WARM_ROWS, 4, P], F32, name="warm_bank")
         quantise_half(2, 0, w1_at[2])
-        quantise_half(3, 0, w1_at[3])
         quantise_half(2, 0, 0)
-        warm_rows = sb.tile([P, WARM_ROWS], U32, name="warm_rows", align_bytes=64)
-        nc.scalar.copy(warm_rows[:], w1_code[:, 0:WARM_ROWS])
+        quantise_half(3, 0, w1_at[3])
         for i in range(WARM_PASSES):
             nc.tensor.matmul_mx(
                 out=warm_bank[:, i % 4, :],
-                lhsT=warm_rows[:].bitcast(FP8X4),
+                lhsT=w1_code[:, 0:WARM_ROWS].bitcast(FP8X4),
                 lhsT_scale=w1_scale[:, 0:WARM_ROWS],
                 rhs=w1_code[:, 0:P].bitcast(FP8X4),
                 rhs_scale=w1_scale[:, 0:P],

@@ -22,7 +22,7 @@ CLOUDS = CHUNK // 2
 ENTRIES = 16
 W2_SCALAR = 72
 W1_VECTOR = 20
-WARM_PASSES = 9
+WARM_PASSES = 10
 WARM_ROWS = 32
 
 
@@ -142,7 +142,7 @@ def tile_picked_ypnseg_max_p_kernel(tc, x_words, x_scales, w1, w2, w3, offs, out
         result = [sb.tile([P, n // 2, 2], F32, name=f"result{g}", align_bytes=64) for g, (j0, n) in enumerate(groups)]
 
         def layer1(c, g, v0):
-            bank = ps.tile([P, 4, CHUNK], F32, name=f"h_bank{c}")
+            bank = ps.tile([P, 4, CHUNK], F32, name=f"h_bank{c}", tag=f"h_bank{c % 3}")
             for t in range(4):
                 nc.tensor.matmul_mx(
                     out=bank[:, t, :],

@@ -15,12 +15,14 @@ FP8X4 = mybir.dt.float8_e4m3fn_x4
 COPY = mybir.ActivationFunctionType.Copy
 RELU = mybir.ActivationFunctionType.Relu
 MAX = mybir.AluOpType.max
+MULT = mybir.AluOpType.mult
+ADD = mybir.AluOpType.add
 
 P = 128
 CHUNK = 128
 CLOUDS = CHUNK // 2
 ENTRIES = 16
-W2_SCALAR = 72
+W2_SCALAR = 64
 W1_VECTOR = 20
 WARM_PASSES = 10
 WARM_ROWS = 32
@@ -121,9 +123,11 @@ def tile_picked_ypnseg_max_p_kernel(tc, x_words, x_scales, w1, w2, w3, offs, out
             return rounded, w23_raw[w][:, :, n0:n1].rearrange("p j (c i) -> p c j i", i=4)
 
         nc.scalar.activation(*w23_views(0, 0, W2_SCALAR), COPY)
-        nc.vector.tensor_copy(*w23_views(0, W2_SCALAR, N))
+        rest = w23_raw[0][:, :, W2_SCALAR:N].rearrange("p j n -> p n j")
+        nc.gpsimd.tensor_scalar(w23_bf[:, 0, W2_SCALAR:N], rest, 1.0, 0.0, MULT, ADD)
         nc.vector.tensor_copy(*w23_views(1, 0, N))
-        quantise(*in_row(w23_at, 2 * N), w23_bf[:].rearrange("p w n j -> p (w n j)"))
+        for w in range(2):
+            quantise(*in_row(w23_at + N * w, N), w23_bf[:, w].rearrange("p n j -> p (n j)"))
 
         groups = [(0, 2 * CHUNK), (2 * CHUNK, CHUNK), (3 * CHUNK, CHUNK)]
         h_first = sb.tile([P, 2, 2 * CLOUDS, 4], BF16, name="h_first", align_bytes=64)

@@ -22,7 +22,6 @@ P = 128
 CHUNK = 128
 CLOUDS = CHUNK // 2
 ENTRIES = 16
-W2_SCALAR = 64
 W1_VECTOR = 20
 WARM_PASSES = 10
 WARM_ROWS = 32
@@ -122,12 +121,8 @@ def tile_picked_ypnseg_max_p_kernel(tc, x_words, x_scales, w1, w2, w3, offs, out
             rounded = w23_bf[:, w, n0:n1].rearrange("p (c i) j -> p c j i", i=4)
             return rounded, w23_raw[w][:, :, n0:n1].rearrange("p j (c i) -> p c j i", i=4)
 
-        nc.scalar.activation(*w23_views(0, 0, W2_SCALAR), COPY)
-        rest = w23_raw[0][:, :, W2_SCALAR:N].rearrange("p j n -> p n j")
-        nc.gpsimd.tensor_scalar(w23_bf[:, 0, W2_SCALAR:N], rest, 1.0, 0.0, MULT, ADD)
-        nc.vector.tensor_copy(*w23_views(1, 0, N))
-        for w in range(2):
-            quantise(*in_row(w23_at + N * w, N), w23_bf[:, w].rearrange("p n j -> p (n j)"))
+        nc.scalar.activation(*w23_views(0, 0, N), COPY)
+        nc.gpsimd.tensor_scalar(w23_bf[:, 1], w23_raw[1][:].rearrange("p j n -> p n j"), 1.0, 0.0, MULT, ADD)
 
         groups = [(0, 2 * CHUNK), (2 * CHUNK, CHUNK), (3 * CHUNK, CHUNK)]
         h_first = sb.tile([P, 2, 2 * CLOUDS, 4], BF16, name="h_first", align_bytes=64)
@@ -145,22 +140,27 @@ def tile_picked_ypnseg_max_p_kernel(tc, x_words, x_scales, w1, w2, w3, offs, out
         z_last_scale = sb.tile([P, CHUNK], U8, name="z_last_scale", align_bytes=64)
         result = [sb.tile([P, n // 2, 2], F32, name=f"result{g}", align_bytes=64) for g, (j0, n) in enumerate(groups)]
 
-        def layer1(c, g, v0):
-            bank = ps.tile([P, 4, CHUNK], F32, name=f"h_bank{c}", tag=f"h_bank{c % 3}")
+        def layer1(c, g, v0, first=0, n=CHUNK, on_vector=False):
+            bank = ps.tile([P, 4, n], F32, name=f"h_bank{c}_{first}", tag=f"h_bank{c % 3}_{first}")
             for t in range(4):
                 nc.tensor.matmul_mx(
                     out=bank[:, t, :],
                     lhsT=w1_code[:, w1_at[t] : w1_at[t] + P].bitcast(FP8X4),
                     lhsT_scale=w1_scale[:, w1_at[t] : w1_at[t] + P],
-                    rhs=x_code[c][:].bitcast(FP8X4),
-                    rhs_scale=x_scale[:, CHUNK * c : CHUNK * (c + 1)],
+                    rhs=x_code[c][:, first : first + n].bitcast(FP8X4),
+                    rhs_scale=x_scale[:, CHUNK * c + first : CHUNK * c + first + n],
                     start=True,
                     stop=True,
                 )
-            nc.scalar.activation(h_bf[g][:, :, v0 : v0 + CLOUDS, :], bank[:].rearrange("p t (v d) -> p d v t", d=2), RELU)
+            rounded = h_bf[g][:, :, v0 : v0 + n // 2, :]
+            sums = bank[:].rearrange("p t (v d) -> p d v t", d=2)
+            if on_vector:
+                nc.vector.tensor_scalar_max(rounded, sums, 0.0)
+            else:
+                nc.scalar.activation(rounded, sums, RELU)
 
-        def pool(g, v0):
-            v = slice(v0, v0 + CLOUDS)
+        def pool(g, clouds):
+            v = slice(0, clouds)
             nc.vector.tensor_tensor(z_bf[g][:, v], h_bf[g][:, 0, v], h_bf[g][:, 1, v], MAX)
 
         def project(sums, w, codes, scales, start, stop):
@@ -175,9 +175,9 @@ def tile_picked_ypnseg_max_p_kernel(tc, x_words, x_scales, w1, w2, w3, offs, out
                 stop=stop,
             )
 
-        def store(g):
+        def store(g, queue):
             j0, n = groups[g]
-            nc.sync.dma_start(out=out[:, j0 : j0 + n], in_=result[g][:].rearrange("p v d -> p (v d)"))
+            queue.dma_start(out=out[:, j0 : j0 + n], in_=result[g][:].rearrange("p v d -> p (v d)"))
 
         def layer2_first():
             bank = ps.tile([P, 2, 2 * CLOUDS], F32, name="out_bank0")
@@ -185,7 +185,7 @@ def tile_picked_ypnseg_max_p_kernel(tc, x_words, x_scales, w1, w2, w3, offs, out
             for d in range(2):
                 project(bank[:, d, :], 1, *in_row(z_first_at, 2 * CLOUDS), False, d == 1)
             nc.scalar.activation(result[0][:], bank[:].rearrange("p d v -> p v d"), COPY)
-            store(0)
+            store(0, nc.sync)
 
         def layer2_third():
             bank = ps.tile([P, 2 * CHUNK], F32, name="out_bank1")
@@ -194,27 +194,28 @@ def tile_picked_ypnseg_max_p_kernel(tc, x_words, x_scales, w1, w2, w3, offs, out
             project(bank[:, CHUNK : 2 * CHUNK], 1, *in_row(z_third_at, CHUNK), False, False)
             project(sums, 0, *in_row(0, CHUNK), False, True)
             nc.scalar.activation(result[1][:], sums.rearrange("p (d v) -> p v d", d=2), COPY)
-            store(1)
+            store(1, nc.scalar)
 
         def layer2_last():
             bank = ps.tile([P, 2, CLOUDS], F32, name="out_bank2")
             project(bank[:].rearrange("p d v -> p (d v)"), 0, h_last_code[:], h_last_scale[:], True, False)
             project(bank[:].rearrange("p d v -> p (d v)"), 1, z_last_code[:], z_last_scale[:], False, True)
             nc.vector.tensor_copy(result[2][:], bank[:].rearrange("p d v -> p v d"))
-            store(2)
+            store(2, nc.sync)
 
         layer1(0, 0, 0)
-        layer1(1, 0, CLOUDS)
+        layer1(1, 0, CLOUDS, 0, CLOUDS, True)
+        layer1(1, 0, CLOUDS + CLOUDS // 2, CLOUDS, CLOUDS)
         layer1(2, 1, 0)
         layer1(3, 2, 0)
-        pool(0, 0)
-        pool(0, CLOUDS)
+        quantise(*in_row(w23_at, 2 * N), w23_bf[:].rearrange("p w n j -> p (w n j)"))
+        pool(0, 2 * CLOUDS)
         quantise(h_first_code[:], h_first_scale[:], h_first[:].rearrange("p d v t -> p (d v t)"))
         quantise(*in_row(z_first_at, 2 * CLOUDS), z_bf[0].rearrange("p v t -> p (v t)"))
-        pool(1, 0)
+        pool(1, CLOUDS)
         quantise(*in_row(0, CHUNK), h_bf[1].rearrange("p d v t -> p (d v t)"))
         quantise(*in_row(z_third_at, CLOUDS), z_third[:].rearrange("p v t -> p (v t)"))
-        pool(2, 0)
+        pool(2, CLOUDS)
         quantise(h_last_code[:], h_last_scale[:], h_last[:].rearrange("p d v t -> p (d v t)"))
         for d in range(2):
             cols = slice(CLOUDS * d, CLOUDS * (d + 1))

@@ -194,7 +194,7 @@ def tile_picked_ypnseg_max_p_kernel(tc, x_words, x_scales, w1, w2, w3, offs, out
             project(bank[:, CHUNK : 2 * CHUNK], 1, *in_row(z_third_at, CHUNK), False, False)
             project(sums, 0, *in_row(0, CHUNK), False, True)
             nc.scalar.activation(result[1][:], sums.rearrange("p (d v) -> p v d", d=2), COPY)
-            store(1, nc.scalar)
+            store(1, nc.sync)
 
         def layer2_last():
             bank = ps.tile([P, 2, CLOUDS], F32, name="out_bank2")
@@ -211,9 +211,8 @@ def tile_picked_ypnseg_max_p_kernel(tc, x_words, x_scales, w1, w2, w3, offs, out
         quantise(*in_row(w23_at, 2 * N), w23_bf[:].rearrange("p w n j -> p (w n j)"))
         pool(0, 2 * CLOUDS)
         quantise(h_first_code[:], h_first_scale[:], h_first[:].rearrange("p d v t -> p (d v t)"))
-        quantise(*in_row(z_first_at, 2 * CLOUDS), z_bf[0].rearrange("p v t -> p (v t)"))
         pool(1, CLOUDS)
-        quantise(*in_row(0, CHUNK), h_bf[1].rearrange("p d v t -> p (d v t)"))
+        quantise(*in_row(0, 2 * CHUNK), h_third_z_first[:].rearrange("p a v t -> p (a v t)"))
         quantise(*in_row(z_third_at, CLOUDS), z_third[:].rearrange("p v t -> p (v t)"))
         pool(2, CLOUDS)
         quantise(h_last_code[:], h_last_scale[:], h_last[:].rearrange("p d v t -> p (d v t)"))

@@ -95,16 +95,19 @@ def tile_picked_ypnseg_max_p_kernel(tc, x_words, x_scales, w1, w2, w3, offs, out
 
         x_code = [sb.tile([P, CHUNK], U32, name=f"x_code{c}", align_bytes=64) for c in range(4)]
 
-        def gather_words(c):
-            columns = CHUNK // ENTRIES
-            nc.vector.tensor_copy(x_code[c][:], word_table[:].indirect(offsets[:, columns * c : columns * (c + 1)]))
+        def gather_words(c, first=0, n=CHUNK):
+            j0 = CHUNK * c + first
+            picked = word_table[:].indirect(offsets[:, j0 // ENTRIES : (j0 + n) // ENTRIES])
+            nc.vector.tensor_copy(x_code[c][:, first : first + n], picked)
 
         first_pair = slice(w1_at[0], w1_at[0] + 2 * P)
         quantise(w1_code[:, first_pair], w1_scale[:, first_pair], w1_bf[0][:].rearrange("p t m j -> p (t m j)"))
         gather_words(0)
         for t in range(2, 4):
             quantise_half(t, 1, w1_at[t] + P // 2)
-        for c in range(1, 4):
+        gather_words(1, 0, CLOUDS)
+        gather_words(1, CLOUDS, CLOUDS)
+        for c in range(2, 4):
             gather_words(c)
 
         z_first_at = CHUNK

from contextlib import ExitStack

import concourse.mybir as mybir

K, T, S, H, N = 512, 1024, 512, 512, 128
FLOPS = 2 * K * H * S + 2 * H * N * S + 2 * H * N * (S // 2)

F32 = mybir.dt.float32
BF16 = mybir.dt.bfloat16
I32 = mybir.dt.int32
U32 = mybir.dt.uint32
U16 = mybir.dt.uint16
U8 = mybir.dt.uint8
FP8X4 = mybir.dt.float8_e4m3fn_x4
COPY = mybir.ActivationFunctionType.Copy
RELU = mybir.ActivationFunctionType.Relu
MAX = mybir.AluOpType.max
MULT = mybir.AluOpType.mult
ADD = mybir.AluOpType.add

P = 128
CHUNK = 128
CLOUDS = CHUNK // 2
ENTRIES = 16
W1_VECTOR = 20
WARM_PASSES = 10
WARM_ROWS = 32


def tile_picked_ypnseg_max_p_kernel(tc, x_words, x_scales, w1, w2, w3, offs, out):
    nc = tc.nc
    with ExitStack() as ctx:
        sb = ctx.enter_context(tc.tile_pool(name="sb", bufs=1))
        ps = ctx.enter_context(tc.psum_pool(name="ps", bufs=1))

        offsets = sb.tile([P, S // ENTRIES], U16, name="offsets")
        word_table = sb.tile([P, T], U32, name="word_table", align_bytes=64)
        scale_table = sb.tile([P, T], U8, name="scale_table", align_bytes=64)
        w1_raw = [sb.tile([P, 4, H // 2], F32, name=f"w1_raw{half}", align_bytes=64) for half in range(2)]
        w23_raw = [sb.tile([P, 4, N], F32, name=f"w23_raw{w}", align_bytes=64) for w in range(2)]

        w1_rows = w1.rearrange("(p j) c -> p j c", j=4)
        nc.vector.memset(scale_table[:].bitcast(I32), 0)
        nc.sync.dma_start(out=w1_raw[0][:], in_=w1_rows[:, :, 0 : H // 2])
        nc.sync.dma_start(offsets[:], offs)
        for r in range(4):
            nc.sync.dma_start(out=scale_table[r:P:32, :].bitcast(I32), in_=x_scales[0, r:16:4, :].bitcast(I32))
        nc.sync.dma_start(out=w1_raw[1][:], in_=w1_rows[:, :, H // 2 : H])
        nc.sync.dma_start(out=word_table[:].bitcast(I32), in_=x_words[0].rearrange("p n t -> p (n t)").bitcast(I32))
        nc.sync.dma_start(out=w23_raw[0][:], in_=w2.rearrange("(p j) c -> p j c", j=4))
        nc.sync.dma_start(out=w23_raw[1][:], in_=w3.rearrange("(p j) c -> p j c", j=4))

        x_scale = sb.tile([P, S], U8, name="x_scale", align_bytes=64)

        w1_bf = [sb.tile([P, 2, P, 4], BF16, name=f"w1_bf{pair}", align_bytes=64) for pair in range(2)]
        w1_at = [P // 2 + 2 * P, P // 2 + 3 * P, P // 2, P // 2 + P]
        w1_code = sb.tile([P, P // 2 + H], U32, name="w1_code", align_bytes=64)
        w1_scale = sb.tile([P, P // 2 + H], U8, name="w1_scale", align_bytes=64)

        def quantise(codes, scales, values):
            nc.vector.quantize_mx(out=codes.bitcast(FP8X4), scales=scales, in_=values)

        def quantise_half(t, half, at):
            cols = slice(at, at + P // 2)
            values = w1_bf[t // 2][:, t % 2, P // 2 * half : P // 2 * (half + 1)].rearrange("p m j -> p (m j)")
            quantise(w1_code[:, cols], w1_scale[:, cols], values)

        def w1_views(half, pair, m0, m1):
            rounded = w1_bf[pair][:, :, P // 2 * half + m0 : P // 2 * half + m1].rearrange("p t m j -> p m j t")
            loaded = w1_raw[half][:].rearrange("p j (m t) -> p m j t", t=4)[:, m0:m1, :, 2 * pair : 2 * pair + 2]
            return rounded, loaded

        nc.vector.tensor_copy(*w1_views(0, 1, 0, P // 2))
        nc.vector.tensor_copy(*w1_views(0, 0, 0, W1_VECTOR))
        nc.scalar.activation(*w1_views(0, 0, W1_VECTOR, P // 2), COPY)

        warm_bank = ps.tile([WARM_ROWS, 4, P], F32, name="warm_bank")
        quantise_half(2, 0, w1_at[2])
        quantise_half(2, 0, 0)
        quantise_half(3, 0, w1_at[3])
        for i in range(WARM_PASSES):
            nc.tensor.matmul_mx(
                out=warm_bank[:, i % 4, :],
                lhsT=w1_code[:, 0:WARM_ROWS].bitcast(FP8X4),
                lhsT_scale=w1_scale[:, 0:WARM_ROWS],
                rhs=w1_code[:, 0:P].bitcast(FP8X4),
                rhs_scale=w1_scale[:, 0:P],
                start=True,
                stop=True,
            )
        nc.vector.tensor_copy(x_scale[:], scale_table[:].indirect(offsets[:]))

        for pair in range(2):
            nc.scalar.activation(*w1_views(1, pair, 0, P // 2), COPY)

        x_code = [sb.tile([P, CHUNK], U32, name=f"x_code{c}", align_bytes=64) for c in range(4)]

        def gather_words(c, first=0, n=CHUNK):
            j0 = CHUNK * c + first
            picked = word_table[:].indirect(offsets[:, j0 // ENTRIES : (j0 + n) // ENTRIES])
            nc.vector.tensor_copy(x_code[c][:, first : first + n], picked)

        first_pair = slice(w1_at[0], w1_at[0] + 2 * P)
        quantise(w1_code[:, first_pair], w1_scale[:, first_pair], w1_bf[0][:].rearrange("p t m j -> p (t m j)"))
        gather_words(0)
        for t in range(2, 4):
            quantise_half(t, 1, w1_at[t] + P // 2)
        gather_words(1, 0, CLOUDS)
        gather_words(1, CLOUDS, CLOUDS)
        for c in range(2, 4):
            gather_words(c)

        z_first_at = CHUNK
        z_third_at = z_first_at + 2 * CLOUDS
        w23_at = z_third_at + CLOUDS
        w23_bf = sb.tile([P, 2, N, 4], BF16, name="w23_bf", align_bytes=64)
        row_code = sb.tile([P, w23_at + 2 * N], U32, name="row_code", align_bytes=64)
        row_scale = sb.tile([P, w23_at + 2 * N], U8, name="row_scale", align_bytes=64)

        def in_row(first, columns):
            return row_code[:, first : first + columns], row_scale[:, first : first + columns]

        def w23_views(w, n0, n1):
            rounded = w23_bf[:, w, n0:n1].rearrange("p (c i) j -> p c j i", i=4)
            return rounded, w23_raw[w][:, :, n0:n1].rearrange("p j (c i) -> p c j i", i=4)

        nc.scalar.activation(*w23_views(0, 0, N), COPY)
        nc.gpsimd.tensor_scalar(w23_bf[:, 1], w23_raw[1][:].rearrange("p j n -> p n j"), 1.0, 0.0, MULT, ADD)

        groups = [(0, 2 * CHUNK), (2 * CHUNK, CHUNK), (3 * CHUNK, CHUNK)]
        h_first = sb.tile([P, 2, 2 * CLOUDS, 4], BF16, name="h_first", align_bytes=64)
        h_third_z_first = sb.tile([P, 2, CHUNK, 4], BF16, name="h_third_z_first", align_bytes=64)
        h_last = sb.tile([P, 2, CLOUDS, 4], BF16, name="h_last", align_bytes=64)
        z_third = sb.tile([P, CLOUDS, 4], BF16, name="z_third", align_bytes=64)
        z_last = sb.tile([P, CLOUDS, 4], BF16, name="z_last", align_bytes=64)
        h_bf = [h_first[:], h_third_z_first[:, 0].rearrange("p (d v) t -> p d v t", d=2), h_last[:]]
        z_bf = [h_third_z_first[:, 1], z_third[:], z_last[:]]
        h_first_code = sb.tile([P, 2 * CHUNK], U32, name="h_first_code", align_bytes=64)
        h_first_scale = sb.tile([P, 2 * CHUNK], U8, name="h_first_scale", align_bytes=64)
        h_last_code = sb.tile([P, CHUNK], U32, name="h_last_code", align_bytes=64)
        h_last_scale = sb.tile([P, CHUNK], U8, name="h_last_scale", align_bytes=64)
        z_last_code = sb.tile([P, CHUNK], U32, name="z_last_code", align_bytes=64)
        z_last_scale = sb.tile([P, CHUNK], U8, name="z_last_scale", align_bytes=64)
        result = [sb.tile([P, n // 2, 2], F32, name=f"result{g}", align_bytes=64) for g, (j0, n) in enumerate(groups)]

        def layer1(c, g, v0, first=0, n=CHUNK, on_vector=False):
            bank = ps.tile([P, 4, n], F32, name=f"h_bank{c}_{first}", tag=f"h_bank{c % 3}_{first}")
            for t in range(4):
                nc.tensor.matmul_mx(
                    out=bank[:, t, :],
                    lhsT=w1_code[:, w1_at[t] : w1_at[t] + P].bitcast(FP8X4),
                    lhsT_scale=w1_scale[:, w1_at[t] : w1_at[t] + P],
                    rhs=x_code[c][:, first : first + n].bitcast(FP8X4),
                    rhs_scale=x_scale[:, CHUNK * c + first : CHUNK * c + first + n],
                    start=True,
                    stop=True,
                )
            rounded = h_bf[g][:, :, v0 : v0 + n // 2, :]
            sums = bank[:].rearrange("p t (v d) -> p d v t", d=2)
            if on_vector:
                nc.vector.tensor_scalar_max(rounded, sums, 0.0)
            else:
                nc.scalar.activation(rounded, sums, RELU)

        def pool(g, clouds):
            v = slice(0, clouds)
            nc.vector.tensor_tensor(z_bf[g][:, v], h_bf[g][:, 0, v], h_bf[g][:, 1, v], MAX)

        def project(sums, w, codes, scales, start, stop):
            weight_code, weight_scale = in_row(w23_at + N * w, N)
            nc.tensor.matmul_mx(
                out=sums,
                lhsT=weight_code.bitcast(FP8X4),
                lhsT_scale=weight_scale,
                rhs=codes.bitcast(FP8X4),
                rhs_scale=scales,
                start=start,
                stop=stop,
            )

        def store(g, queue):
            j0, n = groups[g]
            queue.dma_start(out=out[:, j0 : j0 + n], in_=result[g][:].rearrange("p v d -> p (v d)"))

        def layer2_first():
            bank = ps.tile([P, 2, 2 * CLOUDS], F32, name="out_bank0")
            project(bank[:].rearrange("p d v -> p (d v)"), 0, h_first_code[:], h_first_scale[:], True, False)
            for d in range(2):
                project(bank[:, d, :], 1, *in_row(z_first_at, 2 * CLOUDS), False, d == 1)
            nc.scalar.activation(result[0][:], bank[:].rearrange("p d v -> p v d"), COPY)
            store(0, nc.sync)

        def layer2_third():
            bank = ps.tile([P, 2 * CHUNK], F32, name="out_bank1")
            sums = bank[:, CLOUDS : CLOUDS + CHUNK]
            project(bank[:, 0:CHUNK], 1, *in_row(z_third_at - CLOUDS, CHUNK), True, False)
            project(bank[:, CHUNK : 2 * CHUNK], 1, *in_row(z_third_at, CHUNK), False, False)
            project(sums, 0, *in_row(0, CHUNK), False, True)
            nc.scalar.activation(result[1][:], sums.rearrange("p (d v) -> p v d", d=2), COPY)
            store(1, nc.sync)

        def layer2_last():
            bank = ps.tile([P, 2, CLOUDS], F32, name="out_bank2")
            project(bank[:].rearrange("p d v -> p (d v)"), 0, h_last_code[:], h_last_scale[:], True, False)
            project(bank[:].rearrange("p d v -> p (d v)"), 1, z_last_code[:], z_last_scale[:], False, True)
            nc.vector.tensor_copy(result[2][:], bank[:].rearrange("p d v -> p v d"))
            store(2, nc.sync)

        layer1(0, 0, 0)
        layer1(1, 0, CLOUDS, 0, CLOUDS, True)
        layer1(1, 0, CLOUDS + CLOUDS // 2, CLOUDS, CLOUDS)
        layer1(2, 1, 0)
        layer1(3, 2, 0)
        quantise(*in_row(w23_at, 2 * N), w23_bf[:].rearrange("p w n j -> p (w n j)"))
        pool(0, 2 * CLOUDS)
        quantise(h_first_code[:], h_first_scale[:], h_first[:].rearrange("p d v t -> p (d v t)"))
        pool(1, CLOUDS)
        quantise(*in_row(0, 2 * CHUNK), h_third_z_first[:].rearrange("p a v t -> p (a v t)"))
        quantise(*in_row(z_third_at, CLOUDS), z_third[:].rearrange("p v t -> p (v t)"))
        pool(2, CLOUDS)
        quantise(h_last_code[:], h_last_scale[:], h_last[:].rearrange("p d v t -> p (d v t)"))
        for d in range(2):
            cols = slice(CLOUDS * d, CLOUDS * (d + 1))
            quantise(z_last_code[:, cols], z_last_scale[:, cols], z_last[:].rearrange("p v t -> p (v t)"))
        layer2_first()
        layer2_third()
        layer2_last()
